import numpy as np
import ml_dtypes


def mxq(x, axis, fmt="e4m3"):
    dtype, down = {"e4m3": (ml_dtypes.float8_e4m3fn, 7), "e5m2": (ml_dtypes.float8_e5m2, 14)}[fmt]
    v = np.moveaxis(np.asarray(x, np.float32).astype(ml_dtypes.bfloat16).astype(np.float64), axis, -1)
    blocks = v.reshape(v.shape[:-1] + (-1, 32))
    amax = np.abs(blocks).max(-1, keepdims=True)
    byte = np.maximum(np.where(amax > 0, np.frexp(amax)[1] - 1 + 127, 0) - down, 1)
    scale = np.exp2(byte - 127.0)
    codes = (blocks / scale).astype(np.float32).astype(dtype).astype(np.float64)
    return np.moveaxis((codes * scale).reshape(v.shape), -1, axis)


WIDE = False


def mx_kscale(k):
    if not WIDE:
        return np.ones(k)
    levels = np.array([10, -10, 5, -5, 0])
    if k % 512:
        return np.exp2(np.random.permutation(np.resize(levels, k // 32))).repeat(32)
    a = np.empty((k // 512, 16))
    for p in range(k // 512):
        a[p, :8] = np.random.permutation(np.resize(levels, 8))
        for g in range(8):
            far = levels[np.abs(levels - a[p, g]) >= 10]
            a[p, g + 8] = far[np.random.randint(len(far))]
    return np.exp2(a.ravel()).repeat(32)


def f64(x):
    return np.asarray(x).astype(np.float64)


def striped(idx):
    return np.tile(idx.reshape(-1, 16).T, (8, 1)).astype(np.uint16)


def unstriped(offs):
    return offs[:16].T.reshape(-1).astype(np.int64)


E2M1 = np.array([0.0, 0.5, 1.0, 1.5, 2.0, 3.0, 4.0, 6.0, -0.0, -0.5, -1.0, -1.5, -2.0, -3.0, -4.0, -6.0])


def pack_fp4(w):
    k, n = w.shape
    w = f64(np.asarray(w, np.float32).astype(ml_dtypes.bfloat16)).reshape(k // 32, 32, n)
    amax = np.abs(w).max(1)
    mant, ex = np.frexp(amax / 6.0)
    byte = np.clip(np.where(amax > 0, np.where(mant > 0.5, ex, ex - 1) + 127, 1), 1, 254)
    scaled = (w * np.exp2(127.0 - byte)[:, None, :]).reshape(k, n).astype(np.float32)
    c = np.ascontiguousarray(scaled.reshape(k // 512, 128, 4, n).transpose(0, 1, 3, 2)).astype(ml_dtypes.float4_e2m1fn).view(np.uint8) & 0xF
    words = (c[..., 0::2] | (c[..., 1::2] << 4)).reshape(k // 512, 128, 2 * n)
    return np.ascontiguousarray(words), np.ascontiguousarray(byte.astype(np.uint8).reshape(k // 512, 16, n))


def unpack_fp4(words, scales):
    g, _, n = scales.shape
    words = np.ascontiguousarray(words).reshape(g, 128, n, 2)
    nib = np.empty((g, 128, n, 4), np.uint8)
    nib[..., 0::2] = words & 0xF
    nib[..., 1::2] = words >> 4
    vals = E2M1[nib] * np.repeat(np.exp2(scales.astype(np.float64) - 127.0), 8, axis=1)[..., None]
    return vals.transpose(0, 1, 3, 2).reshape(g * 512, n)


def sigmoid(v):
    return 1.0 / (1.0 + np.exp(-np.maximum(v, -700.0)))


K, T, S, N, U = 1024, 2048, 1024, 256, 2048


def setup_inputs():
    n = np.random.standard_normal
    s = mx_kscale(K)[:, None]
    packed_xT = pack_fp4(n((K, T)) * s)
    return {
        "x_words": packed_xT[0],
        "x_scales": packed_xT[1],
        "mem": n((N, U)).astype(np.float32),
        "w1": (n((K, N)) / np.sqrt(K) / s).astype(np.float32),
        "offs": striped(np.random.permutation(T)[:S]),
        "slot": striped(np.random.permutation(U)[:S]),
    }


def reference(x_words, x_scales, mem, w1, offs, slot):
    xq = unpack_fp4(x_words, x_scales)[:, unstriped(offs)]
    y = mxq(f64(w1), 0, "e4m3").T @ xq
    out = f64(mem).copy()
    out[:, unstriped(slot)] = f64(mem)[:, unstriped(slot)] * sigmoid(y)
    return out

@@ -1,0 +1,116 @@
+from contextlib import ExitStack
+
+import concourse.mybir as mybir
+
+K, T, S, N, U = 1024, 2048, 1024, 256, 2048
+FLOPS = 2 * K * S * N
+
+F32 = mybir.dt.float32
+BF16 = mybir.dt.bfloat16
+I32 = mybir.dt.int32
+U32 = mybir.dt.uint32
+U16 = mybir.dt.uint16
+U8 = mybir.dt.uint8
+FP8X4 = mybir.dt.float8_e4m3fn_x4
+FP4X4 = mybir.dt.float4_e2m1fn_x4
+SIGMOID = mybir.ActivationFunctionType.Sigmoid
+MULT = mybir.AluOpType.mult
+
+P = 128
+PACK = 4
+PASSES = K // (P * PACK)
+HALF = 512
+HALVES = S // HALF
+BLOCKS = N // P
+LIST_COLS = HALF // 16
+
+
+def tile_picked_idxput_gate_p_kernel(tc, x_words, x_scales, mem, w1, offs, slot, out):
+    nc = tc.nc
+    with ExitStack() as ctx:
+        keep = ctx.enter_context(tc.tile_pool(name="keep", bufs=1))
+        psum = ctx.enter_context(tc.psum_pool(name="psum", bufs=1))
+
+        offs_sb = keep.tile([P, S // 16], U16, name="offs_sb")
+        slot_sb = keep.tile([P, S // 16], U16, name="slot_sb")
+        scale_table = keep.tile([P, T], U8, name="scale_table", tag="first", align_bytes=64)
+        word_table = [keep.tile([P, T], U16, name=f"word_table{z}", tag=f"words{z}", align_bytes=64) for z in range(PASSES)]
+        w_raw = [keep.tile([P, PACK, N], F32, name=f"w_raw{z}", align_bytes=64) for z in range(PASSES)]
+        picked_scales = keep.tile([P, S], U8, name="picked_scales", align_bytes=64)
+        x_scale = keep.tile([P, PASSES * S], U8, name="x_scale", align_bytes=64)
+
+        warm = keep.tile([P, 2], F32, name="warm")
+        nc.vector.memset(warm[:, 0:1], 0.0)
+        nc.scalar.activation(warm[:, 1:2], warm[:, 0:1], SIGMOID)
+        nc.vector.memset(scale_table[32:64, :].bitcast(I32), 0)
+        nc.vector.memset(scale_table[64:128, :].bitcast(I32), 0)
+        nc.vector.memset(x_scale[:].bitcast(I32), 0)
+        nc.sync.dma_start(offs_sb[:], offs)
+        nc.sync.dma_start(scale_table[0:32, :].bitcast(I32), x_scales.rearrange("z q c -> (z q) c").bitcast(I32))
+        nc.sync.dma_start(slot_sb[:], slot)
+        for z in range(PASSES):
+            nc.sync.dma_start(word_table[z][:].bitcast(I32), x_words[z].bitcast(I32))
+            nc.sync.dma_start(w_raw[z][:], w1[z * 512 : (z + 1) * 512, :].rearrange("(p j) n -> p j n", j=PACK))
+
+        nc.vector.tensor_copy(picked_scales[:], scale_table[:].indirect(offs_sb[:]))
+        for z in range(PASSES):
+            for q in range(4):
+                nc.sync.dma_start(
+                    x_scale[32 * q : 32 * q + 4, z * S : (z + 1) * S].bitcast(I32),
+                    picked_scales[16 * z + 4 * q : 16 * z + 4 * q + 4, :].bitcast(I32),
+                )
+        store = [keep.tile([P, U], F32, name="store0", tag="first", align_bytes=64)]
+        nc.scalar.dma_start(store[0][:], mem[0:P, :])
+
+        picked_words = {}
+        for z in range(PASSES):
+            for h in range(HALVES):
+                picked_words[z, h] = keep.tile([P, HALF], U16, name=f"picked_words{z}{h}", align_bytes=64)
+                nc.vector.tensor_copy(
+                    picked_words[z, h][:],
+                    word_table[z][:].indirect(offs_sb[:, h * LIST_COLS : (h + 1) * LIST_COLS]),
+                )
+
+        store.append(keep.tile([P, U], F32, name="store1", tag="words0", align_bytes=64))
+        nc.sync.dma_start(store[1][:], mem[P : 2 * P, :])
+
+        w_codes, w_scale = [], []
+        for z in range(PASSES):
+            grouped = keep.tile([P, N, PACK], BF16, name=f"grouped{z}", align_bytes=64)
+            nc.scalar.copy(grouped[:], w_raw[z][:].rearrange("p j n -> p n j"))
+            codes = keep.tile([P, N], U32, name=f"w_codes{z}", align_bytes=64)
+            scales = keep.tile([P, N], U8, name=f"w_scales{z}", align_bytes=64)
+            nc.vector.quantize_mx(codes[:].bitcast(FP8X4), scales[:], grouped[:].rearrange("p n j -> p (n j)"))
+            w_codes.append(codes)
+            w_scale.append(scales)
+
+        gate = {}
+        for b in range(BLOCKS):
+            rows = slice(b * P, (b + 1) * P)
+            for h in range(HALVES):
+                acc = psum.tile([P, HALF], F32, name=f"acc{b}{h}")
+                for z in range(PASSES):
+                    nc.tensor.matmul_mx(
+                        out=acc[:],
+                        lhsT=w_codes[z][:, rows].bitcast(FP8X4),
+                        lhsT_scale=w_scale[z][:, rows],
+                        rhs=picked_words[z, h][:].bitcast(FP4X4),
+                        rhs_scale=x_scale[:, z * S + h * HALF : z * S + (h + 1) * HALF],
+                        start=(z == 0),
+                        stop=(z == PASSES - 1),
+                    )
+                gate[b, h] = keep.tile([P, HALF], F32, name=f"gate{b}{h}", align_bytes=64)
+                nc.scalar.activation(gate[b, h][:], acc[:], SIGMOID)
+        old = []
+        for b in range(BLOCKS):
+            old.append(keep.tile([P, S], F32, name=f"old{b}", align_bytes=64))
+            nc.vector.tensor_copy(old[b][:], store[b][:].indirect(slot_sb[:]))
+        for b in range(BLOCKS):
+            for h in range(HALVES):
+                nc.vector.tensor_tensor(
+                    store[b][:].indirect(slot_sb[:, h * LIST_COLS : (h + 1) * LIST_COLS]),
+                    old[b][:, h * HALF : (h + 1) * HALF],
+                    gate[b, h][:],
+                    MULT,
+                )
+            nc.sync.dma_start(out[b * P : (b + 1) * P, :], store[b][:])

@@ -35,35 +35,35 @@ def tile_picked_idxput_gate_p_kernel(tc, x_words, x_scales, mem, w1, offs, slot,
         slot_sb = keep.tile([P, S // 16], U16, name="slot_sb")
         scale_table = keep.tile([P, T], U8, name="scale_table", tag="first", align_bytes=64)
         word_table = [keep.tile([P, T], U16, name=f"word_table{z}", tag=f"words{z}", align_bytes=64) for z in range(PASSES)]
-        w_raw = [keep.tile([P, PACK, N], F32, name=f"w_raw{z}", align_bytes=64) for z in range(PASSES)]
+        w_rows = [w1[z * 512 : (z + 1) * 512, :].rearrange("(p j) n -> p j n", j=PACK) for z in range(PASSES)]
+        w_raw = [keep.tile([P, PACK, N], F32, name="w_raw0", align_bytes=64)]
+        store = [keep.tile([P, U], F32, name="store0", align_bytes=64)]
         picked_scales = keep.tile([P, S], U8, name="picked_scales", align_bytes=64)
         x_scale = keep.tile([P, PASSES * S], U8, name="x_scale", align_bytes=64)
 
+        nc.vector.memset(scale_table[0:96, :].bitcast(I32), 0)
+        nc.gpsimd.memset(x_scale[:].bitcast(I32), 0)
+        nc.sync.dma_start(offs_sb[:], offs)
+        nc.scalar.dma_start(scale_table[96:128, :].bitcast(I32), x_scales.rearrange("z q c -> (z q) c").bitcast(I32))
+        nc.sync.dma_start(slot_sb[:], slot)
         warm = keep.tile([P, 2], F32, name="warm")
         nc.vector.memset(warm[:, 0:1], 0.0)
         nc.scalar.activation(warm[:, 1:2], warm[:, 0:1], SIGMOID)
-        nc.vector.memset(scale_table[32:64, :].bitcast(I32), 0)
-        nc.vector.memset(scale_table[64:128, :].bitcast(I32), 0)
-        nc.vector.memset(x_scale[:].bitcast(I32), 0)
-        nc.sync.dma_start(offs_sb[:], offs)
-        nc.sync.dma_start(scale_table[0:32, :].bitcast(I32), x_scales.rearrange("z q c -> (z q) c").bitcast(I32))
-        nc.sync.dma_start(slot_sb[:], slot)
         for z in range(PASSES):
             nc.sync.dma_start(word_table[z][:].bitcast(I32), x_words[z].bitcast(I32))
-            nc.sync.dma_start(w_raw[z][:], w1[z * 512 : (z + 1) * 512, :].rearrange("(p j) n -> p j n", j=PACK))
+        nc.sync.dma_start(w_raw[0][:], w_rows[0])
+        nc.sync.dma_start(store[0][:], mem[0:P, :])
 
-        nc.vector.tensor_copy(picked_scales[:], scale_table[:].indirect(offs_sb[:]))
-        for z in range(PASSES):
+        def place_scales(z):
             for q in range(4):
                 nc.sync.dma_start(
                     x_scale[32 * q : 32 * q + 4, z * S : (z + 1) * S].bitcast(I32),
-                    picked_scales[16 * z + 4 * q : 16 * z + 4 * q + 4, :].bitcast(I32),
+                    picked_scales[96 + 16 * z + 4 * q : 96 + 16 * z + 4 * q + 4, :].bitcast(I32),
                 )
-        store = [keep.tile([P, U], F32, name="store0", tag="first", align_bytes=64)]
-        nc.scalar.dma_start(store[0][:], mem[0:P, :])
 
         picked_words = {}
-        for z in range(PASSES):
+
+        def pick_words(z):
             for h in range(HALVES):
                 picked_words[z, h] = keep.tile([P, HALF], U16, name=f"picked_words{z}{h}", align_bytes=64)
                 nc.vector.tensor_copy(
@@ -71,8 +71,15 @@ def tile_picked_idxput_gate_p_kernel(tc, x_words, x_scales, mem, w1, offs, slot,
                     word_table[z][:].indirect(offs_sb[:, h * LIST_COLS : (h + 1) * LIST_COLS]),
                 )
 
+        nc.vector.tensor_copy(picked_scales[:], scale_table[:].indirect(offs_sb[:]))
+        pick_words(0)
+        place_scales(0)
+        w_raw.append(keep.tile([P, PACK, N], F32, name="w_raw1", tag="first", align_bytes=64))
+        nc.sync.dma_start(w_raw[1][:], w_rows[1])
         store.append(keep.tile([P, U], F32, name="store1", tag="words0", align_bytes=64))
         nc.sync.dma_start(store[1][:], mem[P : 2 * P, :])
+        place_scales(1)
+        pick_words(1)
 
         w_codes, w_scale = [], []
         for z in range(PASSES):
@@ -84,9 +91,10 @@ def tile_picked_idxput_gate_p_kernel(tc, x_words, x_scales, mem, w1, offs, slot,
             w_codes.append(codes)
             w_scale.append(scales)
 
-        gate = {}
+        gate = []
         for b in range(BLOCKS):
             rows = slice(b * P, (b + 1) * P)
+            gate.append(keep.tile([P, S], F32, name=f"gate{b}", align_bytes=64))
             for h in range(HALVES):
                 acc = psum.tile([P, HALF], F32, name=f"acc{b}{h}")
                 for z in range(PASSES):
@@ -99,18 +107,11 @@ def tile_picked_idxput_gate_p_kernel(tc, x_words, x_scales, mem, w1, offs, slot,
                         start=(z == 0),
                         stop=(z == PASSES - 1),
                     )
-                gate[b, h] = keep.tile([P, HALF], F32, name=f"gate{b}{h}", align_bytes=64)
-                nc.scalar.activation(gate[b, h][:], acc[:], SIGMOID)
+                nc.scalar.activation(gate[b][:, h * HALF : (h + 1) * HALF], acc[:], SIGMOID)
         old = []
         for b in range(BLOCKS):
             old.append(keep.tile([P, S], F32, name=f"old{b}", align_bytes=64))
             nc.vector.tensor_copy(old[b][:], store[b][:].indirect(slot_sb[:]))
         for b in range(BLOCKS):
-            for h in range(HALVES):
-                nc.vector.tensor_tensor(
-                    store[b][:].indirect(slot_sb[:, h * LIST_COLS : (h + 1) * LIST_COLS]),
-                    old[b][:, h * HALF : (h + 1) * HALF],
-                    gate[b, h][:],
-                    MULT,
-                )
+            nc.vector.tensor_tensor(store[b][:].indirect(slot_sb[:]), old[b][:], gate[b][:], MULT)
             nc.sync.dma_start(out[b * P : (b + 1) * P, :], store[b][:])

@@ -22,7 +22,6 @@ PASSES = K // (P * PACK)
 HALF = 512
 HALVES = S // HALF
 BLOCKS = N // P
-LIST_COLS = HALF // 16
 
 
 def tile_picked_idxput_gate_p_kernel(tc, x_words, x_scales, mem, w1, offs, slot, out):
@@ -34,9 +33,9 @@ def tile_picked_idxput_gate_p_kernel(tc, x_words, x_scales, mem, w1, offs, slot,
         offs_sb = keep.tile([P, S // 16], U16, name="offs_sb")
         slot_sb = keep.tile([P, S // 16], U16, name="slot_sb")
         scale_table = keep.tile([P, T], U8, name="scale_table", tag="first", align_bytes=64)
-        word_table = [keep.tile([P, T], U16, name=f"word_table{z}", tag=f"words{z}", align_bytes=64) for z in range(PASSES)]
+        word_table = [keep.tile([P, 2 * T], U16, name=f"word_table{z}", align_bytes=64) for z in range(PASSES)]
         w_rows = [w1[z * 512 : (z + 1) * 512, :].rearrange("(p j) n -> p j n", j=PACK) for z in range(PASSES)]
-        w_raw = [keep.tile([P, PACK, N], F32, name="w_raw0", align_bytes=64)]
+        w_raw = [keep.tile([P, PACK, N], F32, name=f"w_raw{z}", align_bytes=64) for z in range(PASSES)]
         store = [keep.tile([P, U], F32, name="store0", align_bytes=64)]
         picked_scales = keep.tile([P, S], U8, name="picked_scales", align_bytes=64)
         x_scale = keep.tile([P, PASSES * S], U8, name="x_scale", align_bytes=64)
@@ -44,70 +43,62 @@ def tile_picked_idxput_gate_p_kernel(tc, x_words, x_scales, mem, w1, offs, slot,
         nc.vector.memset(scale_table[0:96, :].bitcast(I32), 0)
         nc.gpsimd.memset(x_scale[:].bitcast(I32), 0)
         nc.sync.dma_start(offs_sb[:], offs)
-        nc.scalar.dma_start(scale_table[96:128, :].bitcast(I32), x_scales.rearrange("z q c -> (z q) c").bitcast(I32))
-        nc.sync.dma_start(slot_sb[:], slot)
+        nc.scalar.dma_start(scale_table[96:128, :].bitcast(I32), x_scales.rearrange("z r c -> r z c").bitcast(I32))
         warm = keep.tile([P, 2], F32, name="warm")
         nc.vector.memset(warm[:, 0:1], 0.0)
         nc.scalar.activation(warm[:, 1:2], warm[:, 0:1], SIGMOID)
         for z in range(PASSES):
-            nc.sync.dma_start(word_table[z][:].bitcast(I32), x_words[z].bitcast(I32))
-        nc.sync.dma_start(w_raw[0][:], w_rows[0])
+            nc.sync.dma_start(word_table[z][:, 0:T].bitcast(I32), x_words[z].bitcast(I32))
+        for z in range(PASSES):
+            nc.sync.dma_start(w_raw[z][:], w_rows[z])
+        nc.sync.dma_start(slot_sb[:], slot)
         nc.sync.dma_start(store[0][:], mem[0:P, :])
 
-        def place_scales(z):
-            for q in range(4):
-                nc.sync.dma_start(
-                    x_scale[32 * q : 32 * q + 4, z * S : (z + 1) * S].bitcast(I32),
-                    picked_scales[96 + 16 * z + 4 * q : 96 + 16 * z + 4 * q + 4, :].bitcast(I32),
-                )
-
-        picked_words = {}
-
-        def pick_words(z):
-            for h in range(HALVES):
-                picked_words[z, h] = keep.tile([P, HALF], U16, name=f"picked_words{z}{h}", align_bytes=64)
-                nc.vector.tensor_copy(
-                    picked_words[z, h][:],
-                    word_table[z][:].indirect(offs_sb[:, h * LIST_COLS : (h + 1) * LIST_COLS]),
-                )
-
         nc.vector.tensor_copy(picked_scales[:], scale_table[:].indirect(offs_sb[:]))
-        pick_words(0)
-        place_scales(0)
-        w_raw.append(keep.tile([P, PACK, N], F32, name="w_raw1", tag="first", align_bytes=64))
-        nc.sync.dma_start(w_raw[1][:], w_rows[1])
-        store.append(keep.tile([P, U], F32, name="store1", tag="words0", align_bytes=64))
-        nc.sync.dma_start(store[1][:], mem[P : 2 * P, :])
-        place_scales(1)
-        pick_words(1)
 
-        w_codes, w_scale = [], []
+        def place_scales(q, cols):
+            nc.sync.dma_start(
+                x_scale[32 * q : 32 * q + 4, :].rearrange("p (z c) -> p z c", z=PASSES)[:, :, cols].bitcast(I32),
+                picked_scales[96 + 8 * q : 96 + 8 * q + 8, cols].bitcast(I32),
+            )
+
+        for q in range(3):
+            place_scales(q, slice(0, S))
+        place_scales(3, slice(0, HALF))
+        store.append(keep.tile([P, U], F32, name="store1", tag="first", align_bytes=64))
+        nc.sync.dma_start(store[1][:], mem[P : 2 * P, :])
+        place_scales(3, slice(HALF, S))
+
+        picked_words = []
         for z in range(PASSES):
-            grouped = keep.tile([P, N, PACK], BF16, name=f"grouped{z}", align_bytes=64)
-            nc.scalar.copy(grouped[:], w_raw[z][:].rearrange("p j n -> p n j"))
-            codes = keep.tile([P, N], U32, name=f"w_codes{z}", align_bytes=64)
-            scales = keep.tile([P, N], U8, name=f"w_scales{z}", align_bytes=64)
-            nc.vector.quantize_mx(codes[:].bitcast(FP8X4), scales[:], grouped[:].rearrange("p n j -> p (n j)"))
-            w_codes.append(codes)
-            w_scale.append(scales)
+            picked_words.append(keep.tile([P, S], U16, name=f"picked_words{z}", align_bytes=64))
+            nc.vector.tensor_copy(picked_words[z][:], word_table[z][:].indirect(offs_sb[:]))
+
+        grouped = keep.tile([P, PASSES, N, PACK], BF16, name="grouped", align_bytes=64)
+        for z in range(PASSES):
+            nc.scalar.copy(grouped[:, z, :, :], w_raw[z][:].rearrange("p j n -> p n j"))
+        w_codes = keep.tile([P, PASSES * N], U32, name="w_codes", align_bytes=64)
+        w_scale = keep.tile([P, PASSES * N], U8, name="w_scale", align_bytes=64)
+        nc.vector.quantize_mx(w_codes[:].bitcast(FP8X4), w_scale[:], grouped[:].rearrange("p z n j -> p (z n j)"))
 
         gate = []
         for b in range(BLOCKS):
-            rows = slice(b * P, (b + 1) * P)
             gate.append(keep.tile([P, S], F32, name=f"gate{b}", align_bytes=64))
             for h in range(HALVES):
+                cols = slice(h * HALF, (h + 1) * HALF)
                 acc = psum.tile([P, HALF], F32, name=f"acc{b}{h}")
                 for z in range(PASSES):
+                    rows = slice(z * N + b * P, z * N + (b + 1) * P)
                     nc.tensor.matmul_mx(
                         out=acc[:],
-                        lhsT=w_codes[z][:, rows].bitcast(FP8X4),
-                        lhsT_scale=w_scale[z][:, rows],
-                        rhs=picked_words[z, h][:].bitcast(FP4X4),
+                        lhsT=w_codes[:, rows].bitcast(FP8X4),
+                        lhsT_scale=w_scale[:, rows],
+                        rhs=picked_words[z][:, cols].bitcast(FP4X4),
                         rhs_scale=x_scale[:, z * S + h * HALF : z * S + (h + 1) * HALF],
                         start=(z == 0),
                         stop=(z == PASSES - 1),
                     )
-                nc.scalar.activation(gate[b][:, h * HALF : (h + 1) * HALF], acc[:], SIGMOID)
+                nc.scalar.activation(gate[b][:, cols], acc[:], SIGMOID)
         old = []
         for b in range(BLOCKS):
             old.append(keep.tile([P, S], F32, name=f"old{b}", align_bytes=64))

@@ -42,8 +42,8 @@ def tile_picked_idxput_gate_p_kernel(tc, x_words, x_scales, mem, w1, offs, slot,
 
         nc.vector.memset(scale_table[0:96, :].bitcast(I32), 0)
         nc.gpsimd.memset(x_scale[:].bitcast(I32), 0)
+        nc.sync.dma_start(scale_table[96:128, :].bitcast(I32), x_scales.rearrange("z r c -> r z c").bitcast(I32))
         nc.sync.dma_start(offs_sb[:], offs)
-        nc.scalar.dma_start(scale_table[96:128, :].bitcast(I32), x_scales.rearrange("z r c -> r z c").bitcast(I32))
         warm = keep.tile([P, 2], F32, name="warm")
         nc.vector.memset(warm[:, 0:1], 0.0)
         nc.scalar.activation(warm[:, 1:2], warm[:, 0:1], SIGMOID)

@@ -18,10 +18,15 @@ MULT = mybir.AluOpType.mult
 
 P = 128
 PACK = 4
-PASSES = K // (P * PACK)
+K_PASS = P * PACK
+PASSES = K // K_PASS
 HALF = 512
 HALVES = S // HALF
-BLOCKS = N // P
+ROW_TILES = N // P
+QUADRANT = 32
+QUADRANTS = P // QUADRANT
+SCALE_ROWS = 4
+TABLE_START = P - PASSES * QUADRANTS * SCALE_ROWS
 
 
 def tile_picked_idxput_gate_p_kernel(tc, x_words, x_scales, mem, w1, offs, slot, out):
@@ -32,42 +37,42 @@ def tile_picked_idxput_gate_p_kernel(tc, x_words, x_scales, mem, w1, offs, slot,
 
         offs_sb = keep.tile([P, S // 16], U16, name="offs_sb")
         slot_sb = keep.tile([P, S // 16], U16, name="slot_sb")
-        scale_table = keep.tile([P, T], U8, name="scale_table", tag="first", align_bytes=64)
-        word_table = [keep.tile([P, 2 * T], U16, name=f"word_table{z}", align_bytes=64) for z in range(PASSES)]
-        w_rows = [w1[z * 512 : (z + 1) * 512, :].rearrange("(p j) n -> p j n", j=PACK) for z in range(PASSES)]
+        scale_table = keep.tile([P, T], U8, name="scale_table", tag="table_then_mem", align_bytes=64)
+        word_table = [keep.tile([P, 4 * S], U16, name=f"word_table{z}", align_bytes=64) for z in range(PASSES)]
         w_raw = [keep.tile([P, PACK, N], F32, name=f"w_raw{z}", align_bytes=64) for z in range(PASSES)]
         store = [keep.tile([P, U], F32, name="store0", align_bytes=64)]
         picked_scales = keep.tile([P, S], U8, name="picked_scales", align_bytes=64)
         x_scale = keep.tile([P, PASSES * S], U8, name="x_scale", align_bytes=64)
 
-        nc.vector.memset(scale_table[0:96, :].bitcast(I32), 0)
+        nc.vector.memset(scale_table[0:TABLE_START, :].bitcast(I32), 0)
         nc.gpsimd.memset(x_scale[:].bitcast(I32), 0)
-        nc.sync.dma_start(scale_table[96:128, :].bitcast(I32), x_scales.rearrange("z r c -> r z c").bitcast(I32))
+
+        nc.sync.dma_start(scale_table[TABLE_START:P, :].bitcast(I32), x_scales.rearrange("z i c -> i z c").bitcast(I32))
         nc.sync.dma_start(offs_sb[:], offs)
-        warm = keep.tile([P, 2], F32, name="warm")
-        nc.vector.memset(warm[:, 0:1], 0.0)
-        nc.scalar.activation(warm[:, 1:2], warm[:, 0:1], SIGMOID)
         for z in range(PASSES):
             nc.sync.dma_start(word_table[z][:, 0:T].bitcast(I32), x_words[z].bitcast(I32))
         for z in range(PASSES):
-            nc.sync.dma_start(w_raw[z][:], w_rows[z])
+            nc.sync.dma_start(w_raw[z][:], w1[z * K_PASS : (z + 1) * K_PASS, :].rearrange("(p t) n -> p t n", t=PACK))
         nc.sync.dma_start(slot_sb[:], slot)
         nc.sync.dma_start(store[0][:], mem[0:P, :])
 
         nc.vector.tensor_copy(picked_scales[:], scale_table[:].indirect(offs_sb[:]))
 
-        def place_scales(q, cols):
+        def place_scales(q, entries):
+            first = TABLE_START + q * SCALE_ROWS * PASSES
+            rows = x_scale[q * QUADRANT : q * QUADRANT + SCALE_ROWS, :]
             nc.sync.dma_start(
-                x_scale[32 * q : 32 * q + 4, :].rearrange("p (z c) -> p z c", z=PASSES)[:, :, cols].bitcast(I32),
-                picked_scales[96 + 8 * q : 96 + 8 * q + 8, cols].bitcast(I32),
+                rows.rearrange("r (z c) -> r z c", z=PASSES)[:, :, entries].bitcast(I32),
+                picked_scales[first : first + SCALE_ROWS * PASSES, entries].bitcast(I32),
             )
 
-        for q in range(3):
+        last = QUADRANTS - 1
+        for q in range(last):
             place_scales(q, slice(0, S))
-        place_scales(3, slice(0, HALF))
-        store.append(keep.tile([P, U], F32, name="store1", tag="first", align_bytes=64))
+        place_scales(last, slice(0, HALF))
+        store.append(keep.tile([P, U], F32, name="store1", tag="table_then_mem", align_bytes=64))
         nc.sync.dma_start(store[1][:], mem[P : 2 * P, :])
-        place_scales(3, slice(HALF, S))
+        place_scales(last, slice(HALF, S))
 
         picked_words = []
         for z in range(PASSES):
@@ -76,33 +81,34 @@ def tile_picked_idxput_gate_p_kernel(tc, x_words, x_scales, mem, w1, offs, slot,
 
         grouped = keep.tile([P, PASSES, N, PACK], BF16, name="grouped", align_bytes=64)
         for z in range(PASSES):
-            nc.scalar.copy(grouped[:, z, :, :], w_raw[z][:].rearrange("p j n -> p n j"))
+            nc.scalar.copy(grouped[:, z, :, :], w_raw[z][:].rearrange("p t n -> p n t"))
         w_codes = keep.tile([P, PASSES * N], U32, name="w_codes", align_bytes=64)
         w_scale = keep.tile([P, PASSES * N], U8, name="w_scale", align_bytes=64)
-        nc.vector.quantize_mx(w_codes[:].bitcast(FP8X4), w_scale[:], grouped[:].rearrange("p z n j -> p (z n j)"))
+        nc.vector.quantize_mx(w_codes[:].bitcast(FP8X4), w_scale[:], grouped[:].rearrange("p z n t -> p (z n t)"))
 
         gate = []
-        for b in range(BLOCKS):
+        for b in range(ROW_TILES):
             gate.append(keep.tile([P, S], F32, name=f"gate{b}", align_bytes=64))
             for h in range(HALVES):
-                cols = slice(h * HALF, (h + 1) * HALF)
+                entries = slice(h * HALF, (h + 1) * HALF)
                 acc = psum.tile([P, HALF], F32, name=f"acc{b}{h}")
                 for z in range(PASSES):
-                    rows = slice(z * N + b * P, z * N + (b + 1) * P)
+                    w_cols = slice(z * N + b * P, z * N + (b + 1) * P)
                     nc.tensor.matmul_mx(
                         out=acc[:],
-                        lhsT=w_codes[:, rows].bitcast(FP8X4),
-                        lhsT_scale=w_scale[:, rows],
-                        rhs=picked_words[z][:, cols].bitcast(FP4X4),
+                        lhsT=w_codes[:, w_cols].bitcast(FP8X4),
+                        lhsT_scale=w_scale[:, w_cols],
+                        rhs=picked_words[z][:, entries].bitcast(FP4X4),
                         rhs_scale=x_scale[:, z * S + h * HALF : z * S + (h + 1) * HALF],
                         start=(z == 0),
                         stop=(z == PASSES - 1),
                     )
-                nc.scalar.activation(gate[b][:, cols], acc[:], SIGMOID)
+                nc.scalar.activation(gate[b][:, entries], acc[:], SIGMOID)
+
         old = []
-        for b in range(BLOCKS):
+        for b in range(ROW_TILES):
             old.append(keep.tile([P, S], F32, name=f"old{b}", align_bytes=64))
             nc.vector.tensor_copy(old[b][:], store[b][:].indirect(slot_sb[:]))
-        for b in range(BLOCKS):
+        for b in range(ROW_TILES):
             nc.vector.tensor_tensor(store[b][:].indirect(slot_sb[:]), old[b][:], gate[b][:], MULT)
             nc.sync.dma_start(out[b * P : (b + 1) * P, :], store[b][:])

@@ -22,6 +22,8 @@ K_PASS = P * PACK
 PASSES = K // K_PASS
 HALF = 512
 HALVES = S // HALF
+LATE = 128
+EARLY = S - LATE
 ROW_TILES = N // P
 QUADRANT = 32
 QUADRANTS = P // QUADRANT
@@ -69,10 +71,10 @@ def tile_picked_idxput_gate_p_kernel(tc, x_words, x_scales, mem, w1, offs, slot,
         last = QUADRANTS - 1
         for q in range(last):
             place_scales(q, slice(0, S))
-        place_scales(last, slice(0, HALF))
+        place_scales(last, slice(0, EARLY))
         store.append(keep.tile([P, U], F32, name="store1", tag="table_then_mem", align_bytes=64))
         nc.sync.dma_start(store[1][:], mem[P : 2 * P, :])
-        place_scales(last, slice(HALF, S))
+        place_scales(last, slice(EARLY, S))
 
         picked_words = []
         for z in range(PASSES):
@@ -86,24 +88,35 @@ def tile_picked_idxput_gate_p_kernel(tc, x_words, x_scales, mem, w1, offs, slot,
         w_scale = keep.tile([P, PASSES * N], U8, name="w_scale", align_bytes=64)
         nc.vector.quantize_mx(w_codes[:].bitcast(FP8X4), w_scale[:], grouped[:].rearrange("p z n t -> p (z n t)"))
 
-        gate = []
-        for b in range(ROW_TILES):
-            gate.append(keep.tile([P, S], F32, name=f"gate{b}", align_bytes=64))
-            for h in range(HALVES):
-                entries = slice(h * HALF, (h + 1) * HALF)
-                acc = psum.tile([P, HALF], F32, name=f"acc{b}{h}")
-                for z in range(PASSES):
-                    w_cols = slice(z * N + b * P, z * N + (b + 1) * P)
-                    nc.tensor.matmul_mx(
-                        out=acc[:],
-                        lhsT=w_codes[:, w_cols].bitcast(FP8X4),
-                        lhsT_scale=w_scale[:, w_cols],
-                        rhs=picked_words[z][:, entries].bitcast(FP4X4),
-                        rhs_scale=x_scale[:, z * S + h * HALF : z * S + (h + 1) * HALF],
-                        start=(z == 0),
-                        stop=(z == PASSES - 1),
-                    )
-                nc.scalar.activation(gate[b][:, entries], acc[:], SIGMOID)
+        def multiply(acc, b, entries):
+            for z in range(PASSES):
+                w_cols = slice(z * N + b * P, z * N + (b + 1) * P)
+                nc.tensor.matmul_mx(
+                    out=acc,
+                    lhsT=w_codes[:, w_cols].bitcast(FP8X4),
+                    lhsT_scale=w_scale[:, w_cols],
+                    rhs=picked_words[z][:, entries].bitcast(FP4X4),
+                    rhs_scale=x_scale[:, z * S + entries.start : z * S + entries.stop],
+                    start=(z == 0),
+                    stop=(z == PASSES - 1),
+                )
+
+        gate = [keep.tile([P, S], F32, name=f"gate{b}", align_bytes=64) for b in range(ROW_TILES)]
+        acc = psum.tile([P, HALF], F32, name="acc_first")
+        multiply(acc[:], 0, slice(0, HALF))
+        nc.scalar.activation(gate[0][:, 0:HALF], acc[:], SIGMOID)
+        acc = psum.tile([P, EARLY - HALF], F32, name="acc_middle")
+        for start in range(HALF, EARLY, LATE):
+            multiply(acc[:, start - HALF : start - HALF + LATE], 0, slice(start, start + LATE))
+        nc.scalar.activation(gate[0][:, HALF:EARLY], acc[:], SIGMOID)
+        acc = psum.tile([P, LATE], F32, name="acc_late", tag="last_bank")
+        multiply(acc[:], 0, slice(EARLY, S))
+        nc.scalar.activation(gate[0][:, EARLY:S], acc[:], SIGMOID)
+        for h in range(HALVES):
+            entries = slice(h * HALF, (h + 1) * HALF)
+            acc = psum.tile([P, HALF], F32, name=f"acc_second{h}", tag="last_bank")
+            multiply(acc[:], 1, entries)
+            nc.scalar.activation(gate[1][:, entries], acc[:], SIGMOID)
 
         old = []
         for b in range(ROW_TILES):

@@ -47,7 +47,7 @@ def tile_picked_idxput_gate_p_kernel(tc, x_words, x_scales, mem, w1, offs, slot,
         x_scale = keep.tile([P, PASSES * S], U8, name="x_scale", align_bytes=64)
 
         nc.vector.memset(scale_table[0:TABLE_START, :].bitcast(I32), 0)
-        nc.gpsimd.memset(x_scale[:].bitcast(I32), 0)
+        nc.vector.memset(x_scale[:].bitcast(I32), 0)
 
         nc.sync.dma_start(scale_table[TABLE_START:P, :].bitcast(I32), x_scales.rearrange("z i c -> i z c").bitcast(I32))
         nc.sync.dma_start(offs_sb[:], offs)

@@ -82,8 +82,8 @@ def tile_picked_idxput_gate_p_kernel(tc, x_words, x_scales, mem, w1, offs, slot,
             nc.vector.tensor_copy(picked_words[z][:], word_table[z][:].indirect(offs_sb[:]))
 
         grouped = keep.tile([P, PASSES, N, PACK], BF16, name="grouped", align_bytes=64)
-        for z in range(PASSES):
-            nc.scalar.copy(grouped[:, z, :, :], w_raw[z][:].rearrange("p t n -> p n t"))
+        nc.gpsimd.tensor_scalar(grouped[:, 0, :, :], w_raw[0][:].rearrange("p t n -> p n t"), 1.0, 0.0, MULT, mybir.AluOpType.add)
+        nc.scalar.copy(grouped[:, 1, :, :], w_raw[1][:].rearrange("p t n -> p n t"))
         w_codes = keep.tile([P, PASSES * N], U32, name="w_codes", align_bytes=64)
         w_scale = keep.tile([P, PASSES * N], U8, name="w_scale", align_bytes=64)
         nc.vector.quantize_mx(w_codes[:].bitcast(FP8X4), w_scale[:], grouped[:].rearrange("p z n t -> p (z n t)"))

@@ -13,22 +13,23 @@ U16 = mybir.dt.uint16
 U8 = mybir.dt.uint8
 FP8X4 = mybir.dt.float8_e4m3fn_x4
 FP4X4 = mybir.dt.float4_e2m1fn_x4
-SIGMOID = mybir.ActivationFunctionType.Sigmoid
+ACT = mybir.ActivationFunctionType
 MULT = mybir.AluOpType.mult
+ADD = mybir.AluOpType.add
 
 P = 128
 PACK = 4
 K_PASS = P * PACK
 PASSES = K // K_PASS
 HALF = 512
-HALVES = S // HALF
-LATE = 128
-EARLY = S - LATE
-ROW_TILES = N // P
+NARROW = 128
+QUARTER = 256
 QUADRANT = 32
 QUADRANTS = P // QUADRANT
 SCALE_ROWS = 4
 TABLE_START = P - PASSES * QUADRANTS * SCALE_ROWS
+REACH = 40.0
+TINY = 2.0**-100
 
 
 def tile_picked_idxput_gate_p_kernel(tc, x_words, x_scales, mem, w1, offs, slot, out):
@@ -37,12 +38,17 @@ def tile_picked_idxput_gate_p_kernel(tc, x_words, x_scales, mem, w1, offs, slot,
         keep = ctx.enter_context(tc.tile_pool(name="keep", bufs=1))
         psum = ctx.enter_context(tc.psum_pool(name="psum", bufs=1))
 
+        first, second = slice(0, HALF), slice(HALF, S)
+
+        def columns(entries):
+            return slice(entries.start // 16, entries.stop // 16)
+
         offs_sb = keep.tile([P, S // 16], U16, name="offs_sb")
         slot_sb = keep.tile([P, S // 16], U16, name="slot_sb")
-        scale_table = keep.tile([P, T], U8, name="scale_table", tag="table_then_mem", align_bytes=64)
-        word_table = [keep.tile([P, 4 * S], U16, name=f"word_table{z}", align_bytes=64) for z in range(PASSES)]
-        w_raw = [keep.tile([P, PACK, N], F32, name=f"w_raw{z}", align_bytes=64) for z in range(PASSES)]
-        store = [keep.tile([P, U], F32, name="store0", align_bytes=64)]
+        scale_table = keep.tile([P, T], U8, name="scale_table", align_bytes=64)
+        word_table0 = keep.tile([P, 4 * S], U16, name="word_table0", tag="words_then_inner", align_bytes=64)
+        word_table1 = keep.tile([P, T], U16, name="word_table1", align_bytes=64)
+        w_raw = [keep.tile([P, PACK, N], F32, name=f"w_raw{z}", tag=f"w_raw{z}", align_bytes=64) for z in range(PASSES)]
         picked_scales = keep.tile([P, S], U8, name="picked_scales", align_bytes=64)
         x_scale = keep.tile([P, PASSES * S], U8, name="x_scale", align_bytes=64)
 
@@ -51,77 +57,125 @@ def tile_picked_idxput_gate_p_kernel(tc, x_words, x_scales, mem, w1, offs, slot,
 
         nc.sync.dma_start(scale_table[TABLE_START:P, :].bitcast(I32), x_scales.rearrange("z i c -> i z c").bitcast(I32))
         nc.sync.dma_start(offs_sb[:], offs)
-        for z in range(PASSES):
-            nc.sync.dma_start(word_table[z][:, 0:T].bitcast(I32), x_words[z].bitcast(I32))
+        nc.sync.dma_start(word_table0[:, 0:T].bitcast(I32), x_words[0].bitcast(I32))
         for z in range(PASSES):
             nc.sync.dma_start(w_raw[z][:], w1[z * K_PASS : (z + 1) * K_PASS, :].rearrange("(p t) n -> p t n", t=PACK))
+        nc.sync.dma_start(word_table1[:].bitcast(I32), x_words[1].bitcast(I32))
         nc.sync.dma_start(slot_sb[:], slot)
-        nc.sync.dma_start(store[0][:], mem[0:P, :])
+        outer = keep.tile([P, U], F32, name="outer", align_bytes=64)
+        halves = (slice(0, U // 2), slice(U // 2, U))
+        for cols in halves:
+            nc.sync.dma_start(outer[:, cols], mem[0:P, cols])
 
         nc.vector.tensor_copy(picked_scales[:], scale_table[:].indirect(offs_sb[:]))
-
-        def place_scales(q, entries):
-            first = TABLE_START + q * SCALE_ROWS * PASSES
+        for q in range(QUADRANTS):
+            start = TABLE_START + q * SCALE_ROWS * PASSES
             rows = x_scale[q * QUADRANT : q * QUADRANT + SCALE_ROWS, :]
-            nc.sync.dma_start(
-                rows.rearrange("r (z c) -> r z c", z=PASSES)[:, :, entries].bitcast(I32),
-                picked_scales[first : first + SCALE_ROWS * PASSES, entries].bitcast(I32),
+            nc.scalar.dma_start(
+                rows.rearrange("r (z c) -> r z c", z=PASSES).bitcast(I32),
+                picked_scales[start : start + SCALE_ROWS * PASSES, :].bitcast(I32),
             )
 
-        last = QUADRANTS - 1
-        for q in range(last):
-            place_scales(q, slice(0, S))
-        place_scales(last, slice(0, EARLY))
-        store.append(keep.tile([P, U], F32, name="store1", tag="table_then_mem", align_bytes=64))
-        nc.sync.dma_start(store[1][:], mem[P : 2 * P, :])
-        place_scales(last, slice(EARLY, S))
+        picked0 = keep.tile([P, S], U16, name="picked0", align_bytes=64)
+        nc.vector.tensor_copy(picked0[:], word_table0[:].indirect(offs_sb[:]))
+        inner = keep.tile([P, U], F32, name="inner", tag="words_then_inner", align_bytes=64)
+        nc.sync.dma_start(inner[:], mem[P : 2 * P, :])
 
-        picked_words = []
+        grouped = keep.tile([P, 2, PASSES, P, PACK], BF16, name="grouped", align_bytes=64)
         for z in range(PASSES):
-            picked_words.append(keep.tile([P, S], U16, name=f"picked_words{z}", align_bytes=64))
-            nc.vector.tensor_copy(picked_words[z][:], word_table[z][:].indirect(offs_sb[:]))
+            nc.gpsimd.tensor_scalar(grouped[:, :, z, :, :], w_raw[z][:].rearrange("p t (b m) -> p b m t", b=2), 1.0, 0.0, MULT, ADD)
+        w_codes, w_scale = [], []
 
-        grouped = keep.tile([P, PASSES, N, PACK], BF16, name="grouped", align_bytes=64)
-        nc.gpsimd.tensor_scalar(grouped[:, 0, :, :], w_raw[0][:].rearrange("p t n -> p n t"), 1.0, 0.0, MULT, mybir.AluOpType.add)
-        nc.scalar.copy(grouped[:, 1, :, :], w_raw[1][:].rearrange("p t n -> p n t"))
-        w_codes = keep.tile([P, PASSES * N], U32, name="w_codes", align_bytes=64)
-        w_scale = keep.tile([P, PASSES * N], U8, name="w_scale", align_bytes=64)
-        nc.vector.quantize_mx(w_codes[:].bitcast(FP8X4), w_scale[:], grouped[:].rearrange("p z n t -> p (z n t)"))
+        def quantize(b, tag):
+            w_codes.append(keep.tile([P, PASSES * P], U32, name=f"w_codes{b}", tag=tag, align_bytes=64))
+            w_scale.append(keep.tile([P, PASSES * P], U8, name=f"w_scale{b}", align_bytes=64))
+            nc.vector.quantize_mx(w_codes[b][:].bitcast(FP8X4), w_scale[b][:], grouped[:, b].rearrange("p z m t -> p (z m t)"))
 
-        def multiply(acc, b, entries):
-            for z in range(PASSES):
-                w_cols = slice(z * N + b * P, z * N + (b + 1) * P)
-                nc.tensor.matmul_mx(
-                    out=acc,
-                    lhsT=w_codes[:, w_cols].bitcast(FP8X4),
-                    lhsT_scale=w_scale[:, w_cols],
-                    rhs=picked_words[z][:, entries].bitcast(FP4X4),
-                    rhs_scale=x_scale[:, z * S + entries.start : z * S + entries.stop],
-                    start=(z == 0),
-                    stop=(z == PASSES - 1),
-                )
+        quantize(0, "w_codes0")
 
-        gate = [keep.tile([P, S], F32, name=f"gate{b}", align_bytes=64) for b in range(ROW_TILES)]
-        acc = psum.tile([P, HALF], F32, name="acc_first")
-        multiply(acc[:], 0, slice(0, HALF))
-        nc.scalar.activation(gate[0][:, 0:HALF], acc[:], SIGMOID)
-        acc = psum.tile([P, EARLY - HALF], F32, name="acc_middle")
-        for start in range(HALF, EARLY, LATE):
-            multiply(acc[:, start - HALF : start - HALF + LATE], 0, slice(start, start + LATE))
-        nc.scalar.activation(gate[0][:, HALF:EARLY], acc[:], SIGMOID)
-        acc = psum.tile([P, LATE], F32, name="acc_late", tag="last_bank")
-        multiply(acc[:], 0, slice(EARLY, S))
-        nc.scalar.activation(gate[0][:, EARLY:S], acc[:], SIGMOID)
-        for h in range(HALVES):
-            entries = slice(h * HALF, (h + 1) * HALF)
-            acc = psum.tile([P, HALF], F32, name=f"acc_second{h}", tag="last_bank")
-            multiply(acc[:], 1, entries)
-            nc.scalar.activation(gate[1][:, entries], acc[:], SIGMOID)
+        picked1 = {
+            first.start: keep.tile([P, HALF], U16, name="picked1_first", align_bytes=64),
+            second.start: keep.tile([P, HALF], U16, name="picked1_second", tag="w_raw1", align_bytes=64),
+        }
+        for entries in (first, second):
+            nc.vector.tensor_copy(picked1[entries.start][:], word_table1[:].indirect(offs_sb[:, columns(entries)]))
 
-        old = []
-        for b in range(ROW_TILES):
-            old.append(keep.tile([P, S], F32, name=f"old{b}", align_bytes=64))
-            nc.vector.tensor_copy(old[b][:], store[b][:].indirect(slot_sb[:]))
-        for b in range(ROW_TILES):
-            nc.vector.tensor_tensor(store[b][:].indirect(slot_sb[:]), old[b][:], gate[b][:], MULT)
-            nc.sync.dma_start(out[b * P : (b + 1) * P, :], store[b][:])
+        def make_tanh(mine, b, entries):
+            count = entries.stop - entries.start
+            width = HALF if count == HALF else NARROW
+            acc = psum.tile([P, count], F32, name=f"acc{b}_{entries.start}")
+            for start in range(entries.start, entries.stop, width):
+                group = slice(start, start + width)
+                base = start // HALF * HALF
+                words = (picked0[:, group], picked1[base][:, start - base : start - base + width])
+                for z in range(PASSES):
+                    w_cols = slice(z * P, (z + 1) * P)
+                    nc.tensor.matmul_mx(
+                        out=acc[:, start - entries.start : start - entries.start + width],
+                        lhsT=w_codes[b][:, w_cols].bitcast(FP8X4),
+                        lhsT_scale=w_scale[b][:, w_cols],
+                        rhs=words[z].bitcast(FP4X4),
+                        rhs_scale=x_scale[:, z * S + start : z * S + start + width],
+                        start=(z == 0),
+                        stop=(z == PASSES - 1),
+                    )
+            nc.scalar.activation(mine, acc[:], ACT.Tanh, scale=0.5)
+
+        def make_gate(gate, b, entries, half):
+            mine = bent[:, b, entries]
+            make_tanh(mine, b, entries)
+            nc.scalar.activation(gate, mine, ACT.Identity, scale=half, bias=half)
+
+        def put(window, entries, old, gate):
+            nc.vector.tensor_tensor(window[:].indirect(slot_sb[:, columns(entries)]), old, gate, MULT)
+
+        part = keep.tile([P, 2], F32, name="part", tag="sum_then_old", align_bytes=64)
+
+        def add_sizes(h, tag):
+            sizes = keep.tile([P, U // 2], BF16, name=f"sizes{h}", tag=tag, align_bytes=64)
+            nc.scalar.activation(sizes[:], outer[:, halves[h]], ACT.Abs, scale=1.0 / REACH, accum_out=part[:, h : h + 1])
+
+        quarters = (slice(0, QUARTER), slice(QUARTER, HALF))
+        gate_first = keep.tile([P, HALF], F32, name="gate_first", align_bytes=64)
+        add_sizes(0, "sizes_then_first")
+        bent_first = keep.tile([P, QUARTER], F32, name="bent_first", align_bytes=64)
+        make_tanh(bent_first[:], 0, quarters[0])
+        nc.gpsimd.tensor_scalar(gate_first[:, quarters[0]], bent_first[:], 0.5, 0.5, MULT, ADD)
+        add_sizes(1, "sizes_then_bent")
+        bent = keep.tile([P, 2, S], F32, name="bent", tag="sizes_then_bent", align_bytes=64)
+
+        old_first = keep.tile([P, HALF], F32, name="old_first", align_bytes=64)
+        for entries in quarters:
+            nc.vector.tensor_copy(old_first[:, entries], outer[:].indirect(slot_sb[:, columns(entries)]))
+        quantize(1, "sizes_then_first")
+        put(outer, quarters[0], old_first[:, quarters[0]], gate_first[:, quarters[0]])
+
+        floored = keep.tile([P, 2], F32, name="floored", align_bytes=64)
+        unit = keep.tile([P, 1], F32, name="unit", align_bytes=64)
+        nc.scalar.activation(floored[:], part[:], ACT.Identity, bias=TINY, accum_out=unit[:])
+        inverse = keep.tile([P, 1], F32, name="inverse", align_bytes=64)
+        nc.vector.reciprocal(inverse[:], unit[:])
+
+        old_inner = keep.tile([P, S], F32, name="old_inner", tag="sum_then_old", align_bytes=64)
+        nc.vector.tensor_copy(old_inner[:], inner[:].indirect(slot_sb[:]))
+        make_gate(gate_first[:, quarters[1]], 0, quarters[1], 0.5)
+        scaled = keep.tile([P, U], F32, name="scaled", align_bytes=64)
+        nc.scalar.activation(scaled[:, halves[0]], outer[:, halves[0]], ACT.Copy, scale=inverse[:])
+        nc.gpsimd.tensor_scalar(scaled[:, halves[1]], outer[:, halves[1]], inverse[:], 0.0, MULT, ADD)
+        put(outer, quarters[1], old_first[:, quarters[1]], gate_first[:, quarters[1]])
+        gate_inner = keep.tile([P, S], F32, name="gate_inner", align_bytes=64)
+        for entries in (first, second):
+            make_gate(gate_inner[:, entries], 1, entries, 0.5)
+        put(inner, slice(0, S), old_inner[:], gate_inner[:])
+        nc.sync.dma_start(out[P : 2 * P, :], inner[:])
+
+        half_unit = keep.tile([P, 1], F32, name="half_unit", align_bytes=64)
+        nc.scalar.activation(half_unit[:], unit[:], ACT.Copy, scale=0.5)
+        gate_unit = keep.tile([P, HALF], F32, name="gate_unit", align_bytes=64)
+        make_gate(gate_unit[:], 0, second, half_unit[:])
+        raised = keep.tile([P, HALF], F32, name="raised", align_bytes=64)
+        nc.scalar.activation(raised[:], scaled[:].indirect(slot_sb[:, columns(second)]), ACT.Exp)
+        old_second = keep.tile([P, HALF], F32, name="old_second", align_bytes=64)
+        nc.scalar.activation(old_second[:], raised[:], ACT.Ln)
+        nc.vector.tensor_tensor(outer[:].indirect(slot_sb[:, columns(second)]), old_second[:], gate_unit[:], MULT)
+        nc.sync.dma_start(out[0:P, :], outer[:])

@@ -22,160 +22,169 @@ PACK = 4
 K_PASS = P * PACK
 PASSES = K // K_PASS
 HALF = 512
-NARROW = 128
-QUARTER = 256
+OPENING = 768
 QUADRANT = 32
 QUADRANTS = P // QUADRANT
 SCALE_ROWS = 4
 TABLE_START = P - PASSES * QUADRANTS * SCALE_ROWS
 REACH = 40.0
 TINY = 2.0**-100
+PIECES = (0, 256, 768, 1408, 2048)
 
 
 def tile_picked_idxput_gate_p_kernel(tc, x_words, x_scales, mem, w1, offs, slot, out):
     nc = tc.nc
     with ExitStack() as ctx:
         keep = ctx.enter_context(tc.tile_pool(name="keep", bufs=1))
+        gate_pool = ctx.enter_context(tc.tile_pool(name="gate_pool", bufs=1))
         psum = ctx.enter_context(tc.psum_pool(name="psum", bufs=1))
 
         first, second = slice(0, HALF), slice(HALF, S)
+        opening, closing = slice(0, OPENING), slice(OPENING, S)
+        middle = slice(HALF, OPENING)
 
         def columns(entries):
             return slice(entries.start // 16, entries.stop // 16)
 
         offs_sb = keep.tile([P, S // 16], U16, name="offs_sb")
         slot_sb = keep.tile([P, S // 16], U16, name="slot_sb")
-        scale_table = keep.tile([P, T], U8, name="scale_table", align_bytes=64)
-        word_table0 = keep.tile([P, 4 * S], U16, name="word_table0", tag="words_then_inner", align_bytes=64)
-        word_table1 = keep.tile([P, T], U16, name="word_table1", align_bytes=64)
-        w_raw = [keep.tile([P, PACK, N], F32, name=f"w_raw{z}", tag=f"w_raw{z}", align_bytes=64) for z in range(PASSES)]
-        picked_scales = keep.tile([P, S], U8, name="picked_scales", align_bytes=64)
+        scale_table = keep.tile([P, T], U8, name="scale_table", tag="table_then_far", align_bytes=64)
+        word_table = [keep.tile([P, 4 * S], U16, name=f"word_table{z}", align_bytes=64) for z in range(PASSES)]
+        picked_scales = keep.tile([P, S], U8, name="picked_scales", tag="scales_then_weights", align_bytes=64)
         x_scale = keep.tile([P, PASSES * S], U8, name="x_scale", align_bytes=64)
 
         nc.vector.memset(scale_table[0:TABLE_START, :].bitcast(I32), 0)
         nc.vector.memset(x_scale[:].bitcast(I32), 0)
 
+        def load_weights(b, tag):
+            raw = keep.tile([P, PASSES, PACK, P], F32, name=f"w_raw{b}", tag=tag, align_bytes=64)
+            for z in range(PASSES):
+                rows = w1[z * K_PASS : (z + 1) * K_PASS, b * P : (b + 1) * P]
+                nc.sync.dma_start(raw[:, z], rows.rearrange("(p t) n -> p t n", t=PACK))
+            return raw
+
         nc.sync.dma_start(scale_table[TABLE_START:P, :].bitcast(I32), x_scales.rearrange("z i c -> i z c").bitcast(I32))
         nc.sync.dma_start(offs_sb[:], offs)
-        nc.sync.dma_start(word_table0[:, 0:T].bitcast(I32), x_words[0].bitcast(I32))
-        for z in range(PASSES):
-            nc.sync.dma_start(w_raw[z][:], w1[z * K_PASS : (z + 1) * K_PASS, :].rearrange("(p t) n -> p t n", t=PACK))
-        nc.sync.dma_start(word_table1[:].bitcast(I32), x_words[1].bitcast(I32))
+        nc.sync.dma_start(word_table[0][:, 0:T].bitcast(I32), x_words[0].bitcast(I32))
+        w_near = load_weights(0, "w_near")
+        nc.sync.dma_start(word_table[1][:, 0:T].bitcast(I32), x_words[1].bitcast(I32))
         nc.sync.dma_start(slot_sb[:], slot)
-        outer = keep.tile([P, U], F32, name="outer", align_bytes=64)
-        halves = (slice(0, U // 2), slice(U // 2, U))
-        for cols in halves:
-            nc.sync.dma_start(outer[:, cols], mem[0:P, cols])
+        near = keep.tile([P, U], F32, name="near", align_bytes=64)
+        nc.sync.dma_start(near[:], mem[0:P, :])
 
         nc.vector.tensor_copy(picked_scales[:], scale_table[:].indirect(offs_sb[:]))
         for q in range(QUADRANTS):
             start = TABLE_START + q * SCALE_ROWS * PASSES
             rows = x_scale[q * QUADRANT : q * QUADRANT + SCALE_ROWS, :]
-            nc.scalar.dma_start(
+            nc.sync.dma_start(
                 rows.rearrange("r (z c) -> r z c", z=PASSES).bitcast(I32),
                 picked_scales[start : start + SCALE_ROWS * PASSES, :].bitcast(I32),
             )
+        far = keep.tile([P, U], F32, name="far", tag="table_then_far", align_bytes=64)
+        pieces = [slice(a, b) for a, b in zip(PIECES[:-1], PIECES[1:])]
+        for cols in pieces:
+            nc.sync.dma_start(far[:, cols], mem[P : 2 * P, cols])
+        w_far = load_weights(1, "scales_then_weights")
 
-        picked0 = keep.tile([P, S], U16, name="picked0", align_bytes=64)
-        nc.vector.tensor_copy(picked0[:], word_table0[:].indirect(offs_sb[:]))
-        inner = keep.tile([P, U], F32, name="inner", tag="words_then_inner", align_bytes=64)
-        nc.sync.dma_start(inner[:], mem[P : 2 * P, :])
+        picked_words = []
 
-        grouped = keep.tile([P, 2, PASSES, P, PACK], BF16, name="grouped", align_bytes=64)
+        def pick_words(z, tag):
+            picked_words.append(keep.tile([P, S], U16, name=f"picked_words{z}", tag=tag, align_bytes=64))
+            nc.vector.tensor_copy(picked_words[z][:], word_table[z][:].indirect(offs_sb[:]))
+
+        pick_words(0, "picked_words0")
+
+        grouped = [keep.tile([P, PASSES, P, PACK], BF16, name=f"grouped{b}", align_bytes=64) for b in range(2)]
         for z in range(PASSES):
-            nc.gpsimd.tensor_scalar(grouped[:, :, z, :, :], w_raw[z][:].rearrange("p t (b m) -> p b m t", b=2), 1.0, 0.0, MULT, ADD)
+            nc.scalar.copy(grouped[0][:, z], w_near[:, z].rearrange("p t m -> p m t"))
         w_codes, w_scale = [], []
 
-        def quantize(b, tag):
-            w_codes.append(keep.tile([P, PASSES * P], U32, name=f"w_codes{b}", tag=tag, align_bytes=64))
+        def quantize(b):
+            w_codes.append(keep.tile([P, PASSES * P], U32, name=f"w_codes{b}", align_bytes=64))
             w_scale.append(keep.tile([P, PASSES * P], U8, name=f"w_scale{b}", align_bytes=64))
-            nc.vector.quantize_mx(w_codes[b][:].bitcast(FP8X4), w_scale[b][:], grouped[:, b].rearrange("p z m t -> p (z m t)"))
+            nc.vector.quantize_mx(w_codes[b][:].bitcast(FP8X4), w_scale[b][:], grouped[b][:].rearrange("p z m t -> p (z m t)"))
 
-        quantize(0, "w_codes0")
+        def multiply(acc, b, z, entries):
+            w_cols = slice(z * P, (z + 1) * P)
+            nc.tensor.matmul_mx(
+                out=acc[:],
+                lhsT=w_codes[b][:, w_cols].bitcast(FP8X4),
+                lhsT_scale=w_scale[b][:, w_cols],
+                rhs=picked_words[z][:, entries].bitcast(FP4X4),
+                rhs_scale=x_scale[:, z * S + entries.start : z * S + entries.stop],
+                start=(z == 0),
+                stop=(z == PASSES - 1),
+            )
 
-        picked1 = {
-            first.start: keep.tile([P, HALF], U16, name="picked1_first", align_bytes=64),
-            second.start: keep.tile([P, HALF], U16, name="picked1_second", tag="w_raw1", align_bytes=64),
-        }
-        for entries in (first, second):
-            nc.vector.tensor_copy(picked1[entries.start][:], word_table1[:].indirect(offs_sb[:, columns(entries)]))
+        def bend(bent, acc):
+            nc.scalar.activation(bent, acc, ACT.Tanh, scale=0.5)
 
-        def make_tanh(mine, b, entries):
-            count = entries.stop - entries.start
-            width = HALF if count == HALF else NARROW
-            acc = psum.tile([P, count], F32, name=f"acc{b}_{entries.start}")
-            for start in range(entries.start, entries.stop, width):
-                group = slice(start, start + width)
-                base = start // HALF * HALF
-                words = (picked0[:, group], picked1[base][:, start - base : start - base + width])
-                for z in range(PASSES):
-                    w_cols = slice(z * P, (z + 1) * P)
-                    nc.tensor.matmul_mx(
-                        out=acc[:, start - entries.start : start - entries.start + width],
-                        lhsT=w_codes[b][:, w_cols].bitcast(FP8X4),
-                        lhsT_scale=w_scale[b][:, w_cols],
-                        rhs=words[z].bitcast(FP4X4),
-                        rhs_scale=x_scale[:, z * S + start : z * S + start + width],
-                        start=(z == 0),
-                        stop=(z == PASSES - 1),
-                    )
-            nc.scalar.activation(mine, acc[:], ACT.Tanh, scale=0.5)
-
-        def make_gate(gate, b, entries, half):
-            mine = bent[:, b, entries]
-            make_tanh(mine, b, entries)
-            nc.scalar.activation(gate, mine, ACT.Identity, scale=half, bias=half)
+        def finish(gate, bent, half):
+            nc.scalar.activation(gate, bent, ACT.Identity, scale=half, bias=half)
 
         def put(window, entries, old, gate):
             nc.vector.tensor_tensor(window[:].indirect(slot_sb[:, columns(entries)]), old, gate, MULT)
 
-        part = keep.tile([P, 2], F32, name="part", tag="sum_then_old", align_bytes=64)
+        pick_words(1, "picked_words1")
+        quantize(0)
+        acc = [[psum.tile([P, HALF], F32, name=f"acc{b}{h}") for h in range(2)] for b in range(2)]
+        for h, entries in enumerate((first, second)):
+            for z in range(PASSES):
+                multiply(acc[0][h], 0, z, entries)
 
-        def add_sizes(h, tag):
-            sizes = keep.tile([P, U // 2], BF16, name=f"sizes{h}", tag=tag, align_bytes=64)
-            nc.scalar.activation(sizes[:], outer[:, halves[h]], ACT.Abs, scale=1.0 / REACH, accum_out=part[:, h : h + 1])
+        old_near = keep.tile([P, S], F32, name="old_near", align_bytes=64)
+        nc.vector.tensor_copy(old_near[:], near[:].indirect(slot_sb[:]))
+        old_far = keep.tile([P, HALF], F32, name="old_far", align_bytes=64)
+        nc.vector.tensor_copy(old_far[:], far[:].indirect(slot_sb[:, columns(first)]))
 
-        quarters = (slice(0, QUARTER), slice(QUARTER, HALF))
-        gate_first = keep.tile([P, HALF], F32, name="gate_first", align_bytes=64)
-        add_sizes(0, "sizes_then_first")
-        bent_first = keep.tile([P, QUARTER], F32, name="bent_first", align_bytes=64)
-        make_tanh(bent_first[:], 0, quarters[0])
-        nc.gpsimd.tensor_scalar(gate_first[:, quarters[0]], bent_first[:], 0.5, 0.5, MULT, ADD)
-        add_sizes(1, "sizes_then_bent")
-        bent = keep.tile([P, 2, S], F32, name="bent", tag="sizes_then_bent", align_bytes=64)
-
-        old_first = keep.tile([P, HALF], F32, name="old_first", align_bytes=64)
-        for entries in quarters:
-            nc.vector.tensor_copy(old_first[:, entries], outer[:].indirect(slot_sb[:, columns(entries)]))
-        quantize(1, "sizes_then_first")
-        put(outer, quarters[0], old_first[:, quarters[0]], gate_first[:, quarters[0]])
-
-        floored = keep.tile([P, 2], F32, name="floored", align_bytes=64)
+        part = gate_pool.tile([P, 16], F32, name="part", offset=4 * U + 2 * HALF - 32, align_bytes=32)
+        sizes = keep.tile([P, U], BF16, name="sizes", align_bytes=64)
+        for h, cols in enumerate(pieces):
+            nc.scalar.activation(sizes[:, cols], far[:, cols], ACT.Abs, scale=0.5 / REACH, accum_out=part[:, h : h + 1])
+        floored = keep.tile([P, len(pieces)], F32, name="floored", align_bytes=64)
         unit = keep.tile([P, 1], F32, name="unit", align_bytes=64)
-        nc.scalar.activation(floored[:], part[:], ACT.Identity, bias=TINY, accum_out=unit[:])
+        nc.scalar.activation(floored[:], part[:, 0 : len(pieces)], ACT.Identity, bias=TINY, accum_out=unit[:])
         inverse = keep.tile([P, 1], F32, name="inverse", align_bytes=64)
         nc.vector.reciprocal(inverse[:], unit[:])
 
-        old_inner = keep.tile([P, S], F32, name="old_inner", tag="sum_then_old", align_bytes=64)
-        nc.vector.tensor_copy(old_inner[:], inner[:].indirect(slot_sb[:]))
-        make_gate(gate_first[:, quarters[1]], 0, quarters[1], 0.5)
-        scaled = keep.tile([P, U], F32, name="scaled", align_bytes=64)
-        nc.scalar.activation(scaled[:, halves[0]], outer[:, halves[0]], ACT.Copy, scale=inverse[:])
-        nc.gpsimd.tensor_scalar(scaled[:, halves[1]], outer[:, halves[1]], inverse[:], 0.0, MULT, ADD)
-        put(outer, quarters[1], old_first[:, quarters[1]], gate_first[:, quarters[1]])
-        gate_inner = keep.tile([P, S], F32, name="gate_inner", align_bytes=64)
-        for entries in (first, second):
-            make_gate(gate_inner[:, entries], 1, entries, 0.5)
-        put(inner, slice(0, S), old_inner[:], gate_inner[:])
-        nc.sync.dma_start(out[P : 2 * P, :], inner[:])
+        for z in range(PASSES):
+            nc.gpsimd.tensor_scalar(grouped[1][:, z], w_far[:, z].rearrange("p t m -> p m t"), 1.0, 0.0, MULT, ADD)
 
-        half_unit = keep.tile([P, 1], F32, name="half_unit", align_bytes=64)
-        nc.scalar.activation(half_unit[:], unit[:], ACT.Copy, scale=0.5)
-        gate_unit = keep.tile([P, HALF], F32, name="gate_unit", align_bytes=64)
-        make_gate(gate_unit[:], 0, second, half_unit[:])
+        quantize(1)
+        for h, entries in enumerate((first, second)):
+            for z in range(PASSES):
+                multiply(acc[1][h], 1, z, entries)
+
+        gate_opening = keep.tile([P, OPENING], F32, name="gate_opening", align_bytes=64)
+        bent_first = gate_pool.tile([P, HALF], F32, name="bent_first", offset=4 * U - 2 * HALF, align_bytes=32)
+        bent_middle = gate_pool.tile([P, OPENING - HALF], F32, name="bent_middle", offset=4 * U + 2 * HALF, align_bytes=32)
+        bend(bent_first[:], acc[0][0][:])
+        bend(bent_middle[:], acc[0][1][:, 0 : OPENING - HALF])
+        finish(gate_opening[:, first], bent_first[:], 0.5)
+        finish(gate_opening[:, middle], bent_middle[:], 0.5)
+        put(near, opening, old_near[:, opening], gate_opening[:])
+
+        scaled = gate_pool.tile([P, U], F32, name="scaled", offset=0, align_bytes=32)
+        nc.scalar.activation(scaled[:], far[:], ACT.Copy, scale=inverse[:])
+
+        bent_far = [keep.tile([P, HALF], F32, name=f"bent_far{h}", tag=f"bent_far{h}", align_bytes=64) for h in range(2)]
+        gate_far = keep.tile([P, S], F32, name="gate_far", align_bytes=64)
+        for h in range(2):
+            bend(bent_far[h][:], acc[1][h][:])
+        finish(gate_far[:, first], bent_far[0][:], 0.5)
+        put(far, first, old_far[:], gate_far[:, first])
+
+        bent_closing = keep.tile([P, S - OPENING], F32, name="bent_closing", tag="bent_far0", align_bytes=64)
+        bend(bent_closing[:], acc[0][1][:, OPENING - HALF : HALF])
         raised = keep.tile([P, HALF], F32, name="raised", align_bytes=64)
-        nc.scalar.activation(raised[:], scaled[:].indirect(slot_sb[:, columns(second)]), ACT.Exp)
-        old_second = keep.tile([P, HALF], F32, name="old_second", align_bytes=64)
-        nc.scalar.activation(old_second[:], raised[:], ACT.Ln)
-        nc.vector.tensor_tensor(outer[:].indirect(slot_sb[:, columns(second)]), old_second[:], gate_unit[:], MULT)
-        nc.sync.dma_start(out[0:P, :], outer[:])
+        nc.scalar.activation(raised[:], scaled[:].indirect(slot_sb[:, columns(second)]), ACT.Exp, scale=0.5)
+        gate_closing = keep.tile([P, S - OPENING], F32, name="gate_closing", align_bytes=64)
+        finish(gate_closing[:], bent_closing[:], 0.5)
+        put(near, closing, old_near[:, closing], gate_closing[:])
+        nc.sync.dma_start(out[0:P, :], near[:])
+
+        lowered = keep.tile([P, HALF], F32, name="lowered", tag="bent_far0", align_bytes=64)
+        nc.scalar.activation(lowered[:], raised[:], ACT.Ln)
+        finish(gate_far[:, second], bent_far[1][:], unit[:])
+        put(far, second, lowered[:], gate_far[:, second])
+        nc.sync.dma_start(out[P : 2 * P, :], far[:])

@@ -29,13 +29,14 @@ SCALE_ROWS = 4
 TABLE_START = P - PASSES * QUADRANTS * SCALE_ROWS
 REACH = 40.0
 TINY = 2.0**-100
-PIECES = (0, 256, 768, 1408, 2048)
+PIECES = (0, 256, 896, 1536, 2048)
 
 
 def tile_picked_idxput_gate_p_kernel(tc, x_words, x_scales, mem, w1, offs, slot, out):
     nc = tc.nc
     with ExitStack() as ctx:
         keep = ctx.enter_context(tc.tile_pool(name="keep", bufs=1))
+        far_pool = ctx.enter_context(tc.tile_pool(name="far_pool", bufs=1))
         gate_pool = ctx.enter_context(tc.tile_pool(name="gate_pool", bufs=1))
         psum = ctx.enter_context(tc.psum_pool(name="psum", bufs=1))
 
@@ -48,25 +49,24 @@ def tile_picked_idxput_gate_p_kernel(tc, x_words, x_scales, mem, w1, offs, slot,
 
         offs_sb = keep.tile([P, S // 16], U16, name="offs_sb")
         slot_sb = keep.tile([P, S // 16], U16, name="slot_sb")
-        scale_table = keep.tile([P, T], U8, name="scale_table", tag="table_then_far", align_bytes=64)
+        scale_table = far_pool.tile([P, T], U8, name="scale_table", offset=4 * U - T // 2, align_bytes=64)
         word_table = [keep.tile([P, 4 * S], U16, name=f"word_table{z}", align_bytes=64) for z in range(PASSES)]
-        picked_scales = keep.tile([P, S], U8, name="picked_scales", tag="scales_then_weights", align_bytes=64)
+        picked_scales = keep.tile([P, S], U8, name="picked_scales", align_bytes=64)
         x_scale = keep.tile([P, PASSES * S], U8, name="x_scale", align_bytes=64)
 
         nc.vector.memset(scale_table[0:TABLE_START, :].bitcast(I32), 0)
         nc.vector.memset(x_scale[:].bitcast(I32), 0)
 
-        def load_weights(b, tag):
-            raw = keep.tile([P, PASSES, PACK, P], F32, name=f"w_raw{b}", tag=tag, align_bytes=64)
-            for z in range(PASSES):
-                rows = w1[z * K_PASS : (z + 1) * K_PASS, b * P : (b + 1) * P]
-                nc.sync.dma_start(raw[:, z], rows.rearrange("(p t) n -> p t n", t=PACK))
-            return raw
+        def load_weights(raw, b, z):
+            rows = w1[z * K_PASS : (z + 1) * K_PASS, b * P : (b + 1) * P]
+            nc.sync.dma_start(raw[:, z], rows.rearrange("(p t) n -> p t n", t=PACK))
 
         nc.sync.dma_start(scale_table[TABLE_START:P, :].bitcast(I32), x_scales.rearrange("z i c -> i z c").bitcast(I32))
         nc.sync.dma_start(offs_sb[:], offs)
         nc.sync.dma_start(word_table[0][:, 0:T].bitcast(I32), x_words[0].bitcast(I32))
-        w_near = load_weights(0, "w_near")
+        w_near = keep.tile([P, PASSES, PACK, P], F32, name="w_near", align_bytes=64)
+        for z in range(PASSES):
+            load_weights(w_near, 0, z)
         nc.sync.dma_start(word_table[1][:, 0:T].bitcast(I32), x_words[1].bitcast(I32))
         nc.sync.dma_start(slot_sb[:], slot)
         near = keep.tile([P, U], F32, name="near", align_bytes=64)
@@ -80,11 +80,13 @@ def tile_picked_idxput_gate_p_kernel(tc, x_words, x_scales, mem, w1, offs, slot,
                 rows.rearrange("r (z c) -> r z c", z=PASSES).bitcast(I32),
                 picked_scales[start : start + SCALE_ROWS * PASSES, :].bitcast(I32),
             )
-        far = keep.tile([P, U], F32, name="far", tag="table_then_far", align_bytes=64)
+        far = far_pool.tile([P, U], F32, name="far", offset=0, align_bytes=64)
         pieces = [slice(a, b) for a, b in zip(PIECES[:-1], PIECES[1:])]
         for cols in pieces:
             nc.sync.dma_start(far[:, cols], mem[P : 2 * P, cols])
-        w_far = load_weights(1, "scales_then_weights")
+        w_far = far_pool.tile([P, PASSES, PACK, P], F32, name="w_far", offset=4 * U, align_bytes=64)
+        for z in range(PASSES):
+            load_weights(w_far, 1, z)
 
         picked_words = []
 
@@ -95,6 +97,10 @@ def tile_picked_idxput_gate_p_kernel(tc, x_words, x_scales, mem, w1, offs, slot,
         pick_words(0, "picked_words0")
 
         grouped = [keep.tile([P, PASSES, P, PACK], BF16, name=f"grouped{b}", align_bytes=64) for b in range(2)]
+        warm = keep.tile([P, 1], F32, name="warm", align_bytes=64)
+        nc.gpsimd.memset(warm[:], 0.0)
+        warmed = keep.tile([P, 1], F32, name="warmed", align_bytes=64)
+        nc.scalar.activation(warmed[:], warm[:], ACT.Sigmoid)
         for z in range(PASSES):
             nc.scalar.copy(grouped[0][:, z], w_near[:, z].rearrange("p t m -> p m t"))
         w_codes, w_scale = [], []
@@ -116,11 +122,8 @@ def tile_picked_idxput_gate_p_kernel(tc, x_words, x_scales, mem, w1, offs, slot,
                 stop=(z == PASSES - 1),
             )
 
-        def bend(bent, acc):
-            nc.scalar.activation(bent, acc, ACT.Tanh, scale=0.5)
-
-        def finish(gate, bent, half):
-            nc.scalar.activation(gate, bent, ACT.Identity, scale=half, bias=half)
+        def make_gate(gate, acc):
+            nc.scalar.activation(gate, acc, ACT.Sigmoid)
 
         def put(window, entries, old, gate):
             nc.vector.tensor_tensor(window[:].indirect(slot_sb[:, columns(entries)]), old, gate, MULT)
@@ -134,57 +137,50 @@ def tile_picked_idxput_gate_p_kernel(tc, x_words, x_scales, mem, w1, offs, slot,
 
         old_near = keep.tile([P, S], F32, name="old_near", align_bytes=64)
         nc.vector.tensor_copy(old_near[:], near[:].indirect(slot_sb[:]))
-        old_far = keep.tile([P, HALF], F32, name="old_far", align_bytes=64)
-        nc.vector.tensor_copy(old_far[:], far[:].indirect(slot_sb[:, columns(first)]))
 
-        part = gate_pool.tile([P, 16], F32, name="part", offset=4 * U + 2 * HALF - 32, align_bytes=32)
-        sizes = keep.tile([P, U], BF16, name="sizes", align_bytes=64)
+        part = gate_pool.tile([P, 16], F32, name="part", offset=4 * HALF - 32, align_bytes=32)
         for h, cols in enumerate(pieces):
-            nc.scalar.activation(sizes[:, cols], far[:, cols], ACT.Abs, scale=0.5 / REACH, accum_out=part[:, h : h + 1])
+            sizes = keep.tile([P, cols.stop - cols.start], BF16, name=f"sizes{h}", tag=f"sizes{h}", align_bytes=64)
+            nc.scalar.activation(sizes[:], far[:, cols], ACT.Abs, scale=1.0 / REACH, accum_out=part[:, h : h + 1])
         floored = keep.tile([P, len(pieces)], F32, name="floored", align_bytes=64)
         unit = keep.tile([P, 1], F32, name="unit", align_bytes=64)
         nc.scalar.activation(floored[:], part[:, 0 : len(pieces)], ACT.Identity, bias=TINY, accum_out=unit[:])
-        inverse = keep.tile([P, 1], F32, name="inverse", align_bytes=64)
+        inverse = keep.tile([P, 1], F32, name="inverse", tag="inverse_then_gate", align_bytes=64)
         nc.vector.reciprocal(inverse[:], unit[:])
+        old_far = gate_pool.tile([P, HALF], F32, name="old_far", offset=0, align_bytes=32)
+        nc.vector.tensor_copy(old_far[:], far[:].indirect(slot_sb[:, columns(first)]))
 
-        for z in range(PASSES):
-            nc.gpsimd.tensor_scalar(grouped[1][:, z], w_far[:, z].rearrange("p t m -> p m t"), 1.0, 0.0, MULT, ADD)
-
+        for z, cols in ((0, slice(0, P)), (1, slice(0, P // 2))):
+            nc.gpsimd.tensor_scalar(grouped[1][:, z, cols], w_far[:, z, :, cols].rearrange("p t m -> p m t"), 1.0, 0.0, MULT, ADD)
+        nc.scalar.copy(grouped[1][:, 1, P // 2 : P], w_far[:, 1, :, P // 2 : P].rearrange("p t m -> p m t"))
         quantize(1)
         for h, entries in enumerate((first, second)):
             for z in range(PASSES):
                 multiply(acc[1][h], 1, z, entries)
 
-        gate_opening = keep.tile([P, OPENING], F32, name="gate_opening", align_bytes=64)
-        bent_first = gate_pool.tile([P, HALF], F32, name="bent_first", offset=4 * U - 2 * HALF, align_bytes=32)
-        bent_middle = gate_pool.tile([P, OPENING - HALF], F32, name="bent_middle", offset=4 * U + 2 * HALF, align_bytes=32)
-        bend(bent_first[:], acc[0][0][:])
-        bend(bent_middle[:], acc[0][1][:, 0 : OPENING - HALF])
-        finish(gate_opening[:, first], bent_first[:], 0.5)
-        finish(gate_opening[:, middle], bent_middle[:], 0.5)
+        gate_opening = gate_pool.tile([P, OPENING], F32, name="gate_opening", offset=4 * HALF, align_bytes=32)
+        make_gate(gate_opening[:, first], acc[0][0][:])
+        make_gate(gate_opening[:, middle], acc[0][1][:, 0 : OPENING - HALF])
         put(near, opening, old_near[:, opening], gate_opening[:])
 
-        scaled = gate_pool.tile([P, U], F32, name="scaled", offset=0, align_bytes=32)
+        scaled = far_pool.tile([P, U], F32, name="scaled", offset=4 * U, align_bytes=64)
         nc.scalar.activation(scaled[:], far[:], ACT.Copy, scale=inverse[:])
 
-        bent_far = [keep.tile([P, HALF], F32, name=f"bent_far{h}", tag=f"bent_far{h}", align_bytes=64) for h in range(2)]
         gate_far = keep.tile([P, S], F32, name="gate_far", align_bytes=64)
-        for h in range(2):
-            bend(bent_far[h][:], acc[1][h][:])
-        finish(gate_far[:, first], bent_far[0][:], 0.5)
+        make_gate(gate_far[:, first], acc[1][0][:])
         put(far, first, old_far[:], gate_far[:, first])
 
-        bent_closing = keep.tile([P, S - OPENING], F32, name="bent_closing", tag="bent_far0", align_bytes=64)
-        bend(bent_closing[:], acc[0][1][:, OPENING - HALF : HALF])
-        raised = keep.tile([P, HALF], F32, name="raised", align_bytes=64)
-        nc.scalar.activation(raised[:], scaled[:].indirect(slot_sb[:, columns(second)]), ACT.Exp, scale=0.5)
-        gate_closing = keep.tile([P, S - OPENING], F32, name="gate_closing", align_bytes=64)
-        finish(gate_closing[:], bent_closing[:], 0.5)
+        gate_closing = keep.tile([P, S - OPENING], F32, name="gate_closing", tag="inverse_then_gate", align_bytes=64)
+        make_gate(gate_closing[:], acc[0][1][:, OPENING - HALF : HALF])
         put(near, closing, old_near[:, closing], gate_closing[:])
         nc.sync.dma_start(out[0:P, :], near[:])
 
-        lowered = keep.tile([P, HALF], F32, name="lowered", tag="bent_far0", align_bytes=64)
+        make_gate(gate_far[:, second], acc[1][1][:])
+        gate_unit = keep.tile([P, HALF], F32, name="gate_unit", align_bytes=64)
+        nc.scalar.activation(gate_unit[:], gate_far[:, second], ACT.Copy, scale=unit[:])
+        raised = keep.tile([P, HALF], F32, name="raised", align_bytes=64)
+        nc.scalar.activation(raised[:], scaled[:].indirect(slot_sb[:, columns(second)]), ACT.Exp)
+        lowered = keep.tile([P, HALF], F32, name="lowered", align_bytes=64)
         nc.scalar.activation(lowered[:], raised[:], ACT.Ln)
-        finish(gate_far[:, second], bent_far[1][:], unit[:])
-        put(far, second, lowered[:], gate_far[:, second])
+        put(far, second, lowered[:], gate_unit[:])
         nc.sync.dma_start(out[P : 2 * P, :], far[:])

@@ -1,3 +1,4 @@
+import math
 from contextlib import ExitStack
 
 import concourse.mybir as mybir
@@ -27,9 +28,10 @@ QUADRANT = 32
 QUADRANTS = P // QUADRANT
 SCALE_ROWS = 4
 TABLE_START = P - PASSES * QUADRANTS * SCALE_ROWS
-REACH = 40.0
+REACH = 30.0
+SHIFT = 57.0
 TINY = 2.0**-100
-PIECES = (0, 256, 896, 1536, 2048)
+PIECES = (0, 640, 1408, 2048)
 
 
 def tile_picked_idxput_gate_p_kernel(tc, x_words, x_scales, mem, w1, offs, slot, out):
@@ -135,8 +137,10 @@ def tile_picked_idxput_gate_p_kernel(tc, x_words, x_scales, mem, w1, offs, slot,
             for z in range(PASSES):
                 multiply(acc[0][h], 0, z, entries)
 
-        old_near = keep.tile([P, S], F32, name="old_near", align_bytes=64)
-        nc.vector.tensor_copy(old_near[:], near[:].indirect(slot_sb[:]))
+        old_opening = keep.tile([P, OPENING], F32, name="old_opening", align_bytes=64)
+        nc.vector.tensor_copy(old_opening[:], near[:].indirect(slot_sb[:, columns(opening)]))
+        old_far = keep.tile([P, HALF], F32, name="old_far", align_bytes=64)
+        nc.vector.tensor_copy(old_far[:], far[:].indirect(slot_sb[:, columns(first)]))
 
         part = gate_pool.tile([P, 16], F32, name="part", offset=4 * HALF - 32, align_bytes=32)
         for h, cols in enumerate(pieces):
@@ -147,8 +151,8 @@ def tile_picked_idxput_gate_p_kernel(tc, x_words, x_scales, mem, w1, offs, slot,
         nc.scalar.activation(floored[:], part[:, 0 : len(pieces)], ACT.Identity, bias=TINY, accum_out=unit[:])
         inverse = keep.tile([P, 1], F32, name="inverse", tag="inverse_then_gate", align_bytes=64)
         nc.vector.reciprocal(inverse[:], unit[:])
-        old_far = gate_pool.tile([P, HALF], F32, name="old_far", offset=0, align_bytes=32)
-        nc.vector.tensor_copy(old_far[:], far[:].indirect(slot_sb[:, columns(first)]))
+        old_closing = gate_pool.tile([P, S - OPENING], F32, name="old_closing", offset=4 * HALF - 4 * (S - OPENING), align_bytes=32)
+        nc.vector.tensor_copy(old_closing[:], near[:].indirect(slot_sb[:, columns(closing)]))
 
         for z, cols in ((0, slice(0, P)), (1, slice(0, P // 2))):
             nc.gpsimd.tensor_scalar(grouped[1][:, z, cols], w_far[:, z, :, cols].rearrange("p t m -> p m t"), 1.0, 0.0, MULT, ADD)
@@ -161,7 +165,7 @@ def tile_picked_idxput_gate_p_kernel(tc, x_words, x_scales, mem, w1, offs, slot,
         gate_opening = gate_pool.tile([P, OPENING], F32, name="gate_opening", offset=4 * HALF, align_bytes=32)
         make_gate(gate_opening[:, first], acc[0][0][:])
         make_gate(gate_opening[:, middle], acc[0][1][:, 0 : OPENING - HALF])
-        put(near, opening, old_near[:, opening], gate_opening[:])
+        put(near, opening, old_opening[:], gate_opening[:])
 
         scaled = far_pool.tile([P, U], F32, name="scaled", offset=4 * U, align_bytes=64)
         nc.scalar.activation(scaled[:], far[:], ACT.Copy, scale=inverse[:])
@@ -172,15 +176,15 @@ def tile_picked_idxput_gate_p_kernel(tc, x_words, x_scales, mem, w1, offs, slot,
 
         gate_closing = keep.tile([P, S - OPENING], F32, name="gate_closing", tag="inverse_then_gate", align_bytes=64)
         make_gate(gate_closing[:], acc[0][1][:, OPENING - HALF : HALF])
-        put(near, closing, old_near[:, closing], gate_closing[:])
+        put(near, closing, old_closing[:], gate_closing[:])
         nc.sync.dma_start(out[0:P, :], near[:])
 
         make_gate(gate_far[:, second], acc[1][1][:])
         gate_unit = keep.tile([P, HALF], F32, name="gate_unit", align_bytes=64)
         nc.scalar.activation(gate_unit[:], gate_far[:, second], ACT.Copy, scale=unit[:])
         raised = keep.tile([P, HALF], F32, name="raised", align_bytes=64)
-        nc.scalar.activation(raised[:], scaled[:].indirect(slot_sb[:, columns(second)]), ACT.Exp)
+        nc.scalar.activation(raised[:], scaled[:].indirect(slot_sb[:, columns(second)]), ACT.Sigmoid, bias=-SHIFT)
         lowered = keep.tile([P, HALF], F32, name="lowered", align_bytes=64)
-        nc.scalar.activation(lowered[:], raised[:], ACT.Ln)
+        nc.scalar.activation(lowered[:], raised[:], ACT.Ln, scale=math.exp(SHIFT))
         put(far, second, lowered[:], gate_unit[:])
         nc.sync.dma_start(out[P : 2 * P, :], far[:])

@@ -23,7 +23,7 @@ PACK = 4
 K_PASS = P * PACK
 PASSES = K // K_PASS
 HALF = 512
-OPENING = 768
+QUARTER = 256
 QUADRANT = 32
 QUADRANTS = P // QUADRANT
 SCALE_ROWS = 4
@@ -43,8 +43,7 @@ def tile_picked_idxput_gate_p_kernel(tc, x_words, x_scales, mem, w1, offs, slot,
         psum = ctx.enter_context(tc.psum_pool(name="psum", bufs=1))
 
         first, second = slice(0, HALF), slice(HALF, S)
-        opening, closing = slice(0, OPENING), slice(OPENING, S)
-        middle = slice(HALF, OPENING)
+        opening, closing = slice(0, QUARTER), slice(QUARTER, HALF)
 
         def columns(entries):
             return slice(entries.start // 16, entries.stop // 16)
@@ -137,12 +136,12 @@ def tile_picked_idxput_gate_p_kernel(tc, x_words, x_scales, mem, w1, offs, slot,
             for z in range(PASSES):
                 multiply(acc[0][h], 0, z, entries)
 
-        old_opening = keep.tile([P, OPENING], F32, name="old_opening", align_bytes=64)
-        nc.vector.tensor_copy(old_opening[:], near[:].indirect(slot_sb[:, columns(opening)]))
+        old_near = keep.tile([P, S], F32, name="old_near", align_bytes=64)
+        nc.vector.tensor_copy(old_near[:], near[:].indirect(slot_sb[:]))
         old_far = keep.tile([P, HALF], F32, name="old_far", align_bytes=64)
         nc.vector.tensor_copy(old_far[:], far[:].indirect(slot_sb[:, columns(first)]))
 
-        part = gate_pool.tile([P, 16], F32, name="part", offset=4 * HALF - 32, align_bytes=32)
+        part = gate_pool.tile([P, 16], F32, name="part", offset=4 * QUARTER - 32, align_bytes=32)
         for h, cols in enumerate(pieces):
             sizes = keep.tile([P, cols.stop - cols.start], BF16, name=f"sizes{h}", tag=f"sizes{h}", align_bytes=64)
             nc.scalar.activation(sizes[:], far[:, cols], ACT.Abs, scale=1.0 / REACH, accum_out=part[:, h : h + 1])
@@ -151,21 +150,20 @@ def tile_picked_idxput_gate_p_kernel(tc, x_words, x_scales, mem, w1, offs, slot,
         nc.scalar.activation(floored[:], part[:, 0 : len(pieces)], ACT.Identity, bias=TINY, accum_out=unit[:])
         inverse = keep.tile([P, 1], F32, name="inverse", tag="inverse_then_gate", align_bytes=64)
         nc.vector.reciprocal(inverse[:], unit[:])
-        old_closing = gate_pool.tile([P, S - OPENING], F32, name="old_closing", offset=4 * HALF - 4 * (S - OPENING), align_bytes=32)
-        nc.vector.tensor_copy(old_closing[:], near[:].indirect(slot_sb[:, columns(closing)]))
 
-        for z, cols in ((0, slice(0, P)), (1, slice(0, P // 2))):
-            nc.gpsimd.tensor_scalar(grouped[1][:, z, cols], w_far[:, z, :, cols].rearrange("p t m -> p m t"), 1.0, 0.0, MULT, ADD)
-        nc.scalar.copy(grouped[1][:, 1, P // 2 : P], w_far[:, 1, :, P // 2 : P].rearrange("p t m -> p m t"))
+        for z in range(PASSES):
+            nc.gpsimd.tensor_scalar(grouped[1][:, z], w_far[:, z].rearrange("p t m -> p m t"), 1.0, 0.0, MULT, ADD)
+
+        gate_opening = gate_pool.tile([P, QUARTER], F32, name="gate_opening", offset=0, align_bytes=32)
+        gate_second = gate_pool.tile([P, HALF], F32, name="gate_second", offset=4 * QUARTER, align_bytes=32)
+        make_gate(gate_opening[:], acc[0][0][:, opening])
+        make_gate(gate_second[:], acc[0][1][:])
+        put(near, opening, old_near[:, opening], gate_opening[:])
         quantize(1)
         for h, entries in enumerate((first, second)):
             for z in range(PASSES):
                 multiply(acc[1][h], 1, z, entries)
-
-        gate_opening = gate_pool.tile([P, OPENING], F32, name="gate_opening", offset=4 * HALF, align_bytes=32)
-        make_gate(gate_opening[:, first], acc[0][0][:])
-        make_gate(gate_opening[:, middle], acc[0][1][:, 0 : OPENING - HALF])
-        put(near, opening, old_opening[:], gate_opening[:])
+        put(near, second, old_near[:, second], gate_second[:])
 
         scaled = far_pool.tile([P, U], F32, name="scaled", offset=4 * U, align_bytes=64)
         nc.scalar.activation(scaled[:], far[:], ACT.Copy, scale=inverse[:])
@@ -174,9 +172,9 @@ def tile_picked_idxput_gate_p_kernel(tc, x_words, x_scales, mem, w1, offs, slot,
         make_gate(gate_far[:, first], acc[1][0][:])
         put(far, first, old_far[:], gate_far[:, first])
 
-        gate_closing = keep.tile([P, S - OPENING], F32, name="gate_closing", tag="inverse_then_gate", align_bytes=64)
-        make_gate(gate_closing[:], acc[0][1][:, OPENING - HALF : HALF])
-        put(near, closing, old_closing[:], gate_closing[:])
+        gate_closing = keep.tile([P, QUARTER], F32, name="gate_closing", tag="inverse_then_gate", align_bytes=64)
+        make_gate(gate_closing[:], acc[0][0][:, closing])
+        put(near, closing, old_near[:, closing], gate_closing[:])
         nc.sync.dma_start(out[0:P, :], near[:])
 
         make_gate(gate_far[:, second], acc[1][1][:])

@@ -39,7 +39,6 @@ def tile_picked_idxput_gate_p_kernel(tc, x_words, x_scales, mem, w1, offs, slot,
     with ExitStack() as ctx:
         keep = ctx.enter_context(tc.tile_pool(name="keep", bufs=1))
         far_pool = ctx.enter_context(tc.tile_pool(name="far_pool", bufs=1))
-        gate_pool = ctx.enter_context(tc.tile_pool(name="gate_pool", bufs=1))
         psum = ctx.enter_context(tc.psum_pool(name="psum", bufs=1))
 
         first, second = slice(0, HALF), slice(HALF, S)
@@ -60,14 +59,14 @@ def tile_picked_idxput_gate_p_kernel(tc, x_words, x_scales, mem, w1, offs, slot,
 
         def load_weights(raw, b, z):
             rows = w1[z * K_PASS : (z + 1) * K_PASS, b * P : (b + 1) * P]
-            nc.sync.dma_start(raw[:, z], rows.rearrange("(p t) n -> p t n", t=PACK))
+            nc.sync.dma_start(raw, rows.rearrange("(p t) n -> p t n", t=PACK))
 
         nc.sync.dma_start(scale_table[TABLE_START:P, :].bitcast(I32), x_scales.rearrange("z i c -> i z c").bitcast(I32))
         nc.sync.dma_start(offs_sb[:], offs)
         nc.sync.dma_start(word_table[0][:, 0:T].bitcast(I32), x_words[0].bitcast(I32))
         w_near = keep.tile([P, PASSES, PACK, P], F32, name="w_near", align_bytes=64)
         for z in range(PASSES):
-            load_weights(w_near, 0, z)
+            load_weights(w_near[:, z], 0, z)
         nc.sync.dma_start(word_table[1][:, 0:T].bitcast(I32), x_words[1].bitcast(I32))
         nc.sync.dma_start(slot_sb[:], slot)
         near = keep.tile([P, U], F32, name="near", align_bytes=64)
@@ -85,9 +84,8 @@ def tile_picked_idxput_gate_p_kernel(tc, x_words, x_scales, mem, w1, offs, slot,
         pieces = [slice(a, b) for a, b in zip(PIECES[:-1], PIECES[1:])]
         for cols in pieces:
             nc.sync.dma_start(far[:, cols], mem[P : 2 * P, cols])
-        w_far = far_pool.tile([P, PASSES, PACK, P], F32, name="w_far", offset=4 * U, align_bytes=64)
-        for z in range(PASSES):
-            load_weights(w_far, 1, z)
+        w_far = [far_pool.tile([P, PACK, P], F32, name="w_far0", offset=4 * U, align_bytes=64)]
+        load_weights(w_far[0][:], 1, 0)
 
         picked_words = []
 
@@ -141,22 +139,27 @@ def tile_picked_idxput_gate_p_kernel(tc, x_words, x_scales, mem, w1, offs, slot,
         old_far = keep.tile([P, HALF], F32, name="old_far", align_bytes=64)
         nc.vector.tensor_copy(old_far[:], far[:].indirect(slot_sb[:, columns(first)]))
 
-        part = gate_pool.tile([P, 16], F32, name="part", offset=4 * QUARTER - 32, align_bytes=32)
+        part = keep.tile([P, len(pieces)], F32, name="part", tag="part_then_gate", align_bytes=64)
         for h, cols in enumerate(pieces):
-            sizes = keep.tile([P, cols.stop - cols.start], BF16, name=f"sizes{h}", tag=f"sizes{h}", align_bytes=64)
+            if h == 0:
+                sizes = far_pool.tile([P, cols.stop - cols.start], BF16, name="sizes0", offset=5 * U, align_bytes=64)
+            else:
+                sizes = keep.tile([P, cols.stop - cols.start], BF16, name=f"sizes{h}", align_bytes=64)
             nc.scalar.activation(sizes[:], far[:, cols], ACT.Abs, scale=1.0 / REACH, accum_out=part[:, h : h + 1])
+        w_far.append(far_pool.tile([P, PACK, P], F32, name="w_far1", offset=5 * U, align_bytes=64))
+        load_weights(w_far[1][:], 1, 1)
         floored = keep.tile([P, len(pieces)], F32, name="floored", align_bytes=64)
         unit = keep.tile([P, 1], F32, name="unit", align_bytes=64)
-        nc.scalar.activation(floored[:], part[:, 0 : len(pieces)], ACT.Identity, bias=TINY, accum_out=unit[:])
+        nc.scalar.activation(floored[:], part[:], ACT.Identity, bias=TINY, accum_out=unit[:])
         inverse = keep.tile([P, 1], F32, name="inverse", tag="inverse_then_gate", align_bytes=64)
         nc.vector.reciprocal(inverse[:], unit[:])
 
-        for z in range(PASSES):
-            nc.gpsimd.tensor_scalar(grouped[1][:, z], w_far[:, z].rearrange("p t m -> p m t"), 1.0, 0.0, MULT, ADD)
+        nc.gpsimd.tensor_scalar(grouped[1][:, 0], w_far[0][:].rearrange("p t m -> p m t"), 1.0, 0.0, MULT, ADD)
 
-        gate_opening = gate_pool.tile([P, QUARTER], F32, name="gate_opening", offset=0, align_bytes=32)
-        gate_second = gate_pool.tile([P, HALF], F32, name="gate_second", offset=4 * QUARTER, align_bytes=32)
+        gate_opening = keep.tile([P, QUARTER], F32, name="gate_opening", tag="part_then_gate", align_bytes=64)
         make_gate(gate_opening[:], acc[0][0][:, opening])
+        nc.scalar.copy(grouped[1][:, 1], w_far[1][:].rearrange("p t m -> p m t"))
+        gate_second = far_pool.tile([P, HALF], F32, name="gate_second", offset=4 * U + U // 2, align_bytes=64)
         make_gate(gate_second[:], acc[0][1][:])
         put(near, opening, old_near[:, opening], gate_opening[:])
         quantize(1)
@@ -165,7 +168,7 @@ def tile_picked_idxput_gate_p_kernel(tc, x_words, x_scales, mem, w1, offs, slot,
                 multiply(acc[1][h], 1, z, entries)
         put(near, second, old_near[:, second], gate_second[:])
 
-        scaled = far_pool.tile([P, U], F32, name="scaled", offset=4 * U, align_bytes=64)
+        scaled = far_pool.tile([P, U], F32, name="scaled", offset=5 * U + U // 2, align_bytes=64)
         nc.scalar.activation(scaled[:], far[:], ACT.Copy, scale=inverse[:])
 
         gate_far = keep.tile([P, S], F32, name="gate_far", align_bytes=64)

@@ -31,7 +31,7 @@ TABLE_START = P - PASSES * QUADRANTS * SCALE_ROWS
 REACH = 30.0
 SHIFT = 57.0
 TINY = 2.0**-100
-PIECES = (0, 640, 1408, 2048)
+PIECES = (0, 512, 1344, 2048)
 
 
 def tile_picked_idxput_gate_p_kernel(tc, x_words, x_scales, mem, w1, offs, slot, out):
@@ -49,7 +49,9 @@ def tile_picked_idxput_gate_p_kernel(tc, x_words, x_scales, mem, w1, offs, slot,
 
         offs_sb = keep.tile([P, S // 16], U16, name="offs_sb")
         slot_sb = keep.tile([P, S // 16], U16, name="slot_sb")
-        scale_table = far_pool.tile([P, T], U8, name="scale_table", offset=4 * U - T // 2, align_bytes=64)
+        far_bytes = 4 * U
+        pass_bytes = 4 * PACK * P
+        scale_table = far_pool.tile([P, T], U8, name="scale_table", offset=far_bytes - T // 2, align_bytes=64)
         word_table = [keep.tile([P, 4 * S], U16, name=f"word_table{z}", align_bytes=64) for z in range(PASSES)]
         picked_scales = keep.tile([P, S], U8, name="picked_scales", align_bytes=64)
         x_scale = keep.tile([P, PASSES * S], U8, name="x_scale", align_bytes=64)
@@ -84,20 +86,20 @@ def tile_picked_idxput_gate_p_kernel(tc, x_words, x_scales, mem, w1, offs, slot,
         pieces = [slice(a, b) for a, b in zip(PIECES[:-1], PIECES[1:])]
         for cols in pieces:
             nc.sync.dma_start(far[:, cols], mem[P : 2 * P, cols])
-        w_far = [far_pool.tile([P, PACK, P], F32, name="w_far0", offset=4 * U, align_bytes=64)]
+        w_far = [far_pool.tile([P, PACK, P], F32, name="w_far0", offset=far_bytes, align_bytes=64)]
         load_weights(w_far[0][:], 1, 0)
 
         picked_words = []
 
-        def pick_words(z, tag):
-            picked_words.append(keep.tile([P, S], U16, name=f"picked_words{z}", tag=tag, align_bytes=64))
+        def pick_words(z):
+            picked_words.append(keep.tile([P, S], U16, name=f"picked_words{z}", align_bytes=64))
             nc.vector.tensor_copy(picked_words[z][:], word_table[z][:].indirect(offs_sb[:]))
 
-        pick_words(0, "picked_words0")
+        pick_words(0)
 
         grouped = [keep.tile([P, PASSES, P, PACK], BF16, name=f"grouped{b}", align_bytes=64) for b in range(2)]
         warm = keep.tile([P, 1], F32, name="warm", align_bytes=64)
-        nc.gpsimd.memset(warm[:], 0.0)
+        nc.vector.memset(warm[:], 0.0)
         warmed = keep.tile([P, 1], F32, name="warmed", align_bytes=64)
         nc.scalar.activation(warmed[:], warm[:], ACT.Sigmoid)
         for z in range(PASSES):
@@ -127,7 +129,7 @@ def tile_picked_idxput_gate_p_kernel(tc, x_words, x_scales, mem, w1, offs, slot,
         def put(window, entries, old, gate):
             nc.vector.tensor_tensor(window[:].indirect(slot_sb[:, columns(entries)]), old, gate, MULT)
 
-        pick_words(1, "picked_words1")
+        pick_words(1)
         quantize(0)
         acc = [[psum.tile([P, HALF], F32, name=f"acc{b}{h}") for h in range(2)] for b in range(2)]
         for h, entries in enumerate((first, second)):
@@ -140,17 +142,18 @@ def tile_picked_idxput_gate_p_kernel(tc, x_words, x_scales, mem, w1, offs, slot,
         nc.vector.tensor_copy(old_far[:], far[:].indirect(slot_sb[:, columns(first)]))
 
         part = keep.tile([P, len(pieces)], F32, name="part", tag="part_then_gate", align_bytes=64)
+        sizes = keep.tile([P, U], BF16, name="sizes", align_bytes=64)
+        leading = far_pool.tile([P, 1], F32, name="leading", offset=far_bytes + pass_bytes, align_bytes=64)
         for h, cols in enumerate(pieces):
+            total = leading[:] if h == 0 else part[:, h : h + 1]
+            nc.scalar.activation(sizes[:, cols], far[:, cols], ACT.Abs, scale=1.0 / REACH, accum_out=total)
             if h == 0:
-                sizes = far_pool.tile([P, cols.stop - cols.start], BF16, name="sizes0", offset=5 * U, align_bytes=64)
-            else:
-                sizes = keep.tile([P, cols.stop - cols.start], BF16, name=f"sizes{h}", align_bytes=64)
-            nc.scalar.activation(sizes[:], far[:, cols], ACT.Abs, scale=1.0 / REACH, accum_out=part[:, h : h + 1])
-        w_far.append(far_pool.tile([P, PACK, P], F32, name="w_far1", offset=5 * U, align_bytes=64))
+                nc.scalar.activation(part[:, 0:1], leading[:], ACT.Identity, bias=TINY)
+        w_far.append(far_pool.tile([P, PACK, P], F32, name="w_far1", offset=far_bytes + pass_bytes, align_bytes=64))
         load_weights(w_far[1][:], 1, 1)
-        floored = keep.tile([P, len(pieces)], F32, name="floored", align_bytes=64)
+        summed = keep.tile([P, len(pieces)], F32, name="summed", align_bytes=64)
         unit = keep.tile([P, 1], F32, name="unit", align_bytes=64)
-        nc.scalar.activation(floored[:], part[:], ACT.Identity, bias=TINY, accum_out=unit[:])
+        nc.scalar.activation(summed[:], part[:], ACT.Identity, accum_out=unit[:])
         inverse = keep.tile([P, 1], F32, name="inverse", tag="inverse_then_gate", align_bytes=64)
         nc.vector.reciprocal(inverse[:], unit[:])
 
@@ -159,7 +162,7 @@ def tile_picked_idxput_gate_p_kernel(tc, x_words, x_scales, mem, w1, offs, slot,
         gate_opening = keep.tile([P, QUARTER], F32, name="gate_opening", tag="part_then_gate", align_bytes=64)
         make_gate(gate_opening[:], acc[0][0][:, opening])
         nc.scalar.copy(grouped[1][:, 1], w_far[1][:].rearrange("p t m -> p m t"))
-        gate_second = far_pool.tile([P, HALF], F32, name="gate_second", offset=4 * U + U // 2, align_bytes=64)
+        gate_second = far_pool.tile([P, HALF], F32, name="gate_second", offset=far_bytes + pass_bytes // 2, align_bytes=64)
         make_gate(gate_second[:], acc[0][1][:])
         put(near, opening, old_near[:, opening], gate_opening[:])
         quantize(1)
@@ -168,7 +171,7 @@ def tile_picked_idxput_gate_p_kernel(tc, x_words, x_scales, mem, w1, offs, slot,
                 multiply(acc[1][h], 1, z, entries)
         put(near, second, old_near[:, second], gate_second[:])
 
-        scaled = far_pool.tile([P, U], F32, name="scaled", offset=5 * U + U // 2, align_bytes=64)
+        scaled = far_pool.tile([P, U], F32, name="scaled", offset=far_bytes + 3 * pass_bytes // 2, align_bytes=64)
         nc.scalar.activation(scaled[:], far[:], ACT.Copy, scale=inverse[:])
 
         gate_far = keep.tile([P, S], F32, name="gate_far", align_bytes=64)

@@ -23,6 +23,7 @@ PACK = 4
 K_PASS = P * PACK
 PASSES = K // K_PASS
 HALF = 512
+SHARE = 448
 QUARTER = 256
 QUADRANT = 32
 QUADRANTS = P // QUADRANT
@@ -42,6 +43,7 @@ def tile_picked_idxput_gate_p_kernel(tc, x_words, x_scales, mem, w1, offs, slot,
         psum = ctx.enter_context(tc.psum_pool(name="psum", bufs=1))
 
         first, second = slice(0, HALF), slice(HALF, S)
+        by_vector, by_scalar = slice(0, SHARE), slice(SHARE, S)
         opening, closing = slice(0, QUARTER), slice(QUARTER, HALF)
 
         def columns(entries):
@@ -138,8 +140,8 @@ def tile_picked_idxput_gate_p_kernel(tc, x_words, x_scales, mem, w1, offs, slot,
 
         old_near = keep.tile([P, S], F32, name="old_near", align_bytes=64)
         nc.vector.tensor_copy(old_near[:], near[:].indirect(slot_sb[:]))
-        old_far = keep.tile([P, HALF], F32, name="old_far", align_bytes=64)
-        nc.vector.tensor_copy(old_far[:], far[:].indirect(slot_sb[:, columns(first)]))
+        old_far = keep.tile([P, SHARE], F32, name="old_far", align_bytes=64)
+        nc.vector.tensor_copy(old_far[:], far[:].indirect(slot_sb[:, columns(by_vector)]))
 
         part = keep.tile([P, len(pieces)], F32, name="part", tag="part_then_gate", align_bytes=64)
         sizes = keep.tile([P, U], BF16, name="sizes", align_bytes=64)
@@ -176,7 +178,7 @@ def tile_picked_idxput_gate_p_kernel(tc, x_words, x_scales, mem, w1, offs, slot,
 
         gate_far = keep.tile([P, S], F32, name="gate_far", align_bytes=64)
         make_gate(gate_far[:, first], acc[1][0][:])
-        put(far, first, old_far[:], gate_far[:, first])
+        put(far, by_vector, old_far[:], gate_far[:, by_vector])
 
         gate_closing = keep.tile([P, QUARTER], F32, name="gate_closing", tag="inverse_then_gate", align_bytes=64)
         make_gate(gate_closing[:], acc[0][0][:, closing])
@@ -184,11 +186,11 @@ def tile_picked_idxput_gate_p_kernel(tc, x_words, x_scales, mem, w1, offs, slot,
         nc.sync.dma_start(out[0:P, :], near[:])
 
         make_gate(gate_far[:, second], acc[1][1][:])
-        gate_unit = keep.tile([P, HALF], F32, name="gate_unit", align_bytes=64)
-        nc.scalar.activation(gate_unit[:], gate_far[:, second], ACT.Copy, scale=unit[:])
-        raised = keep.tile([P, HALF], F32, name="raised", align_bytes=64)
-        nc.scalar.activation(raised[:], scaled[:].indirect(slot_sb[:, columns(second)]), ACT.Sigmoid, bias=-SHIFT)
-        lowered = keep.tile([P, HALF], F32, name="lowered", align_bytes=64)
+        gate_unit = keep.tile([P, S - SHARE], F32, name="gate_unit", align_bytes=64)
+        nc.scalar.activation(gate_unit[:], gate_far[:, by_scalar], ACT.Copy, scale=unit[:])
+        raised = keep.tile([P, S - SHARE], F32, name="raised", align_bytes=64)
+        nc.scalar.activation(raised[:], scaled[:].indirect(slot_sb[:, columns(by_scalar)]), ACT.Sigmoid, bias=-SHIFT)
+        lowered = keep.tile([P, S - SHARE], F32, name="lowered", align_bytes=64)
         nc.scalar.activation(lowered[:], raised[:], ACT.Ln, scale=math.exp(SHIFT))
-        put(far, second, lowered[:], gate_unit[:])
+        put(far, by_scalar, lowered[:], gate_unit[:])
         nc.sync.dma_start(out[P : 2 * P, :], far[:])

@@ -32,7 +32,7 @@ TABLE_START = P - PASSES * QUADRANTS * SCALE_ROWS
 REACH = 30.0
 SHIFT = 57.0
 TINY = 2.0**-100
-PIECES = (0, 512, 1344, 2048)
+PIECES = (0, 448, 1280, 2048)
 
 
 def tile_picked_idxput_gate_p_kernel(tc, x_words, x_scales, mem, w1, offs, slot, out):
@@ -180,16 +180,17 @@ def tile_picked_idxput_gate_p_kernel(tc, x_words, x_scales, mem, w1, offs, slot,
         make_gate(gate_far[:, first], acc[1][0][:])
         put(far, by_vector, old_far[:], gate_far[:, by_vector])
 
+        raised = keep.tile([P, S - SHARE], F32, name="raised", align_bytes=64)
+        nc.scalar.activation(raised[:], scaled[:].indirect(slot_sb[:, columns(by_scalar)]), ACT.Sigmoid, bias=-SHIFT)
+        make_gate(gate_far[:, second], acc[1][1][:])
+
         gate_closing = keep.tile([P, QUARTER], F32, name="gate_closing", tag="inverse_then_gate", align_bytes=64)
         make_gate(gate_closing[:], acc[0][0][:, closing])
         put(near, closing, old_near[:, closing], gate_closing[:])
         nc.sync.dma_start(out[0:P, :], near[:])
 
-        make_gate(gate_far[:, second], acc[1][1][:])
         gate_unit = keep.tile([P, S - SHARE], F32, name="gate_unit", align_bytes=64)
         nc.scalar.activation(gate_unit[:], gate_far[:, by_scalar], ACT.Copy, scale=unit[:])
-        raised = keep.tile([P, S - SHARE], F32, name="raised", align_bytes=64)
-        nc.scalar.activation(raised[:], scaled[:].indirect(slot_sb[:, columns(by_scalar)]), ACT.Sigmoid, bias=-SHIFT)
         lowered = keep.tile([P, S - SHARE], F32, name="lowered", align_bytes=64)
         nc.scalar.activation(lowered[:], raised[:], ACT.Ln, scale=math.exp(SHIFT))
         put(far, by_scalar, lowered[:], gate_unit[:])

@@ -1,4 +1,3 @@
-import math
 from contextlib import ExitStack
 
 import concourse.mybir as mybir
@@ -22,59 +21,43 @@ P = 128
 PACK = 4
 K_PASS = P * PACK
 PASSES = K // K_PASS
-HALF = 512
-SHARE = 448
-QUARTER = 256
 QUADRANT = 32
 QUADRANTS = P // QUADRANT
 SCALE_ROWS = 4
 TABLE_START = P - PASSES * QUADRANTS * SCALE_ROWS
-REACH = 30.0
-SHIFT = 57.0
-TINY = 2.0**-100
-PIECES = (0, 448, 1280, 2048)
 
 
 def tile_picked_idxput_gate_p_kernel(tc, x_words, x_scales, mem, w1, offs, slot, out):
     nc = tc.nc
     with ExitStack() as ctx:
         keep = ctx.enter_context(tc.tile_pool(name="keep", bufs=1))
-        far_pool = ctx.enter_context(tc.tile_pool(name="far_pool", bufs=1))
+        rows_pool = ctx.enter_context(tc.tile_pool(name="rows_pool", bufs=1))
         psum = ctx.enter_context(tc.psum_pool(name="psum", bufs=1))
-
-        first, second = slice(0, HALF), slice(HALF, S)
-        by_vector, by_scalar = slice(0, SHARE), slice(SHARE, S)
-        opening, closing = slice(0, QUARTER), slice(QUARTER, HALF)
 
         def columns(entries):
             return slice(entries.start // 16, entries.stop // 16)
 
         offs_sb = keep.tile([P, S // 16], U16, name="offs_sb")
         slot_sb = keep.tile([P, S // 16], U16, name="slot_sb")
-        far_bytes = 4 * U
-        pass_bytes = 4 * PACK * P
-        scale_table = far_pool.tile([P, T], U8, name="scale_table", offset=far_bytes - T // 2, align_bytes=64)
-        word_table = [keep.tile([P, 4 * S], U16, name=f"word_table{z}", align_bytes=64) for z in range(PASSES)]
+        row_bytes = 4 * U
+        scale_table = rows_pool.tile([P, T], U8, name="scale_table", offset=row_bytes - T // 2, align_bytes=64)
+        word_table = [
+            keep.tile([P, 4 * S], U16, name="word_table0", align_bytes=64),
+            keep.tile([P, T], U16, name="word_table1", align_bytes=64),
+        ]
         picked_scales = keep.tile([P, S], U8, name="picked_scales", align_bytes=64)
         x_scale = keep.tile([P, PASSES * S], U8, name="x_scale", align_bytes=64)
-
         nc.vector.memset(scale_table[0:TABLE_START, :].bitcast(I32), 0)
         nc.vector.memset(x_scale[:].bitcast(I32), 0)
 
-        def load_weights(raw, b, z):
-            rows = w1[z * K_PASS : (z + 1) * K_PASS, b * P : (b + 1) * P]
-            nc.sync.dma_start(raw, rows.rearrange("(p t) n -> p t n", t=PACK))
-
+        w_raw = [keep.tile([P, PACK, N], F32, name=f"w_raw{z}", tag=f"w_raw{z}", align_bytes=64) for z in range(PASSES)]
         nc.sync.dma_start(scale_table[TABLE_START:P, :].bitcast(I32), x_scales.rearrange("z i c -> i z c").bitcast(I32))
         nc.sync.dma_start(offs_sb[:], offs)
         nc.sync.dma_start(word_table[0][:, 0:T].bitcast(I32), x_words[0].bitcast(I32))
-        w_near = keep.tile([P, PASSES, PACK, P], F32, name="w_near", align_bytes=64)
         for z in range(PASSES):
-            load_weights(w_near[:, z], 0, z)
-        nc.sync.dma_start(word_table[1][:, 0:T].bitcast(I32), x_words[1].bitcast(I32))
+            nc.sync.dma_start(w_raw[z][:], w1[z * K_PASS : (z + 1) * K_PASS, :].rearrange("(p t) n -> p t n", t=PACK))
+        nc.sync.dma_start(word_table[1][:].bitcast(I32), x_words[1].bitcast(I32))
         nc.sync.dma_start(slot_sb[:], slot)
-        near = keep.tile([P, U], F32, name="near", align_bytes=64)
-        nc.sync.dma_start(near[:], mem[0:P, :])
 
         nc.vector.tensor_copy(picked_scales[:], scale_table[:].indirect(offs_sb[:]))
         for q in range(QUADRANTS):
@@ -84,114 +67,92 @@ def tile_picked_idxput_gate_p_kernel(tc, x_words, x_scales, mem, w1, offs, slot,
                 rows.rearrange("r (z c) -> r z c", z=PASSES).bitcast(I32),
                 picked_scales[start : start + SCALE_ROWS * PASSES, :].bitcast(I32),
             )
-        far = far_pool.tile([P, U], F32, name="far", offset=0, align_bytes=64)
-        pieces = [slice(a, b) for a, b in zip(PIECES[:-1], PIECES[1:])]
-        for cols in pieces:
-            nc.sync.dma_start(far[:, cols], mem[P : 2 * P, cols])
-        w_far = [far_pool.tile([P, PACK, P], F32, name="w_far0", offset=far_bytes, align_bytes=64)]
-        load_weights(w_far[0][:], 1, 0)
+        near = rows_pool.tile([P, U], F32, name="near", offset=0, align_bytes=64)
+        far = rows_pool.tile([P, U], F32, name="far", offset=row_bytes, align_bytes=64)
+        nc.sync.dma_start(near[:], mem[0:P, :])
+        nc.sync.dma_start(far[:], mem[P : 2 * P, :])
 
-        picked_words = []
-
-        def pick_words(z):
-            picked_words.append(keep.tile([P, S], U16, name=f"picked_words{z}", align_bytes=64))
-            nc.vector.tensor_copy(picked_words[z][:], word_table[z][:].indirect(offs_sb[:]))
-
-        pick_words(0)
+        picked_words = [keep.tile([P, S], U16, name="picked_words0", align_bytes=64)]
+        nc.vector.tensor_copy(picked_words[0][:], word_table[0][:].indirect(offs_sb[:]))
 
         grouped = [keep.tile([P, PASSES, P, PACK], BF16, name=f"grouped{b}", align_bytes=64) for b in range(2)]
         warm = keep.tile([P, 1], F32, name="warm", align_bytes=64)
         nc.vector.memset(warm[:], 0.0)
         warmed = keep.tile([P, 1], F32, name="warmed", align_bytes=64)
         nc.scalar.activation(warmed[:], warm[:], ACT.Sigmoid)
-        for z in range(PASSES):
-            nc.scalar.copy(grouped[0][:, z], w_near[:, z].rearrange("p t m -> p m t"))
-        w_codes, w_scale = [], []
-
-        def quantize(b):
-            w_codes.append(keep.tile([P, PASSES * P], U32, name=f"w_codes{b}", align_bytes=64))
-            w_scale.append(keep.tile([P, PASSES * P], U8, name=f"w_scale{b}", align_bytes=64))
-            nc.vector.quantize_mx(w_codes[b][:].bitcast(FP8X4), w_scale[b][:], grouped[b][:].rearrange("p z m t -> p (z m t)"))
-
-        def multiply(acc, b, z, entries):
-            w_cols = slice(z * P, (z + 1) * P)
-            nc.tensor.matmul_mx(
-                out=acc[:],
-                lhsT=w_codes[b][:, w_cols].bitcast(FP8X4),
-                lhsT_scale=w_scale[b][:, w_cols],
-                rhs=picked_words[z][:, entries].bitcast(FP4X4),
-                rhs_scale=x_scale[:, z * S + entries.start : z * S + entries.stop],
-                start=(z == 0),
-                stop=(z == PASSES - 1),
+        def cast(b, z):
+            nc.scalar.copy(
+                grouped[b][:, z].rearrange("p (c i) t -> p c t i", i=4),
+                w_raw[z][:, :, b * P : (b + 1) * P].rearrange("p t (c i) -> p c t i", i=4),
             )
 
-        def make_gate(gate, acc):
-            nc.scalar.activation(gate, acc, ACT.Sigmoid)
+        cast(0, 0)
+        nc.gpsimd.tensor_scalar(grouped[1][:, 0], w_raw[0][:, :, P:N].rearrange("p t m -> p m t"), 1.0, 0.0, MULT, ADD)
+        cast(0, 1)
+        cast(1, 1)
+        w_codes = [keep.tile([P, PASSES * P], U32, name=f"w_codes{b}", tag=f"w_codes{b}", align_bytes=64) for b in range(2)]
+        w_scale = [keep.tile([P, PASSES * P], U8, name=f"w_scale{b}", align_bytes=64) for b in range(2)]
+        for b in range(2):
+            nc.vector.quantize_mx(w_codes[b][:].bitcast(FP8X4), w_scale[b][:], grouped[b][:].rearrange("p z m t -> p (z m t)"))
 
-        def put(window, entries, old, gate):
-            nc.vector.tensor_tensor(window[:].indirect(slot_sb[:, columns(entries)]), old, gate, MULT)
+        halves = (slice(0, 512), slice(512, 1024))
+        picked_late = []
+        for h, entries in enumerate(halves):
+            picked_late.append(keep.tile([P, 512], U16, name=f"picked_late{h}", tag=f"w_raw{1 - h}", align_bytes=64))
+            nc.vector.tensor_copy(picked_late[h][:], word_table[1][:].indirect(offs_sb[:, columns(entries)]))
 
-        pick_words(1)
-        quantize(0)
-        acc = [[psum.tile([P, HALF], F32, name=f"acc{b}{h}") for h in range(2)] for b in range(2)]
-        for h, entries in enumerate((first, second)):
-            for z in range(PASSES):
-                multiply(acc[0][h], 0, z, entries)
+        def multiply(acc, b, h):
+            entries = halves[h]
+            for z, words in enumerate((picked_words[0][:, entries], picked_late[h][:])):
+                w_cols = slice(z * P, (z + 1) * P)
+                nc.tensor.matmul_mx(
+                    out=acc[:],
+                    lhsT=w_codes[b][:, w_cols].bitcast(FP8X4),
+                    lhsT_scale=w_scale[b][:, w_cols],
+                    rhs=words.bitcast(FP4X4),
+                    rhs_scale=x_scale[:, z * S + entries.start : z * S + entries.stop],
+                    start=(z == 0),
+                    stop=(z == PASSES - 1),
+                )
 
-        old_near = keep.tile([P, S], F32, name="old_near", align_bytes=64)
-        nc.vector.tensor_copy(old_near[:], near[:].indirect(slot_sb[:]))
-        old_far = keep.tile([P, SHARE], F32, name="old_far", align_bytes=64)
-        nc.vector.tensor_copy(old_far[:], far[:].indirect(slot_sb[:, columns(by_vector)]))
+        acc = [[psum.tile([P, 512], F32, name=f"acc{b}{h}") for h in range(2)] for b in range(2)]
+        for h in range(2):
+            for b in range(2):
+                multiply(acc[b][h], b, h)
 
-        part = keep.tile([P, len(pieces)], F32, name="part", tag="part_then_gate", align_bytes=64)
-        sizes = keep.tile([P, U], BF16, name="sizes", align_bytes=64)
-        leading = far_pool.tile([P, 1], F32, name="leading", offset=far_bytes + pass_bytes, align_bytes=64)
-        for h, cols in enumerate(pieces):
-            total = leading[:] if h == 0 else part[:, h : h + 1]
-            nc.scalar.activation(sizes[:, cols], far[:, cols], ACT.Abs, scale=1.0 / REACH, accum_out=total)
-            if h == 0:
-                nc.scalar.activation(part[:, 0:1], leading[:], ACT.Identity, bias=TINY)
-        w_far.append(far_pool.tile([P, PACK, P], F32, name="w_far1", offset=far_bytes + pass_bytes, align_bytes=64))
-        load_weights(w_far[1][:], 1, 1)
-        summed = keep.tile([P, len(pieces)], F32, name="summed", align_bytes=64)
-        unit = keep.tile([P, 1], F32, name="unit", align_bytes=64)
-        nc.scalar.activation(summed[:], part[:], ACT.Identity, accum_out=unit[:])
-        inverse = keep.tile([P, 1], F32, name="inverse", tag="inverse_then_gate", align_bytes=64)
-        nc.vector.reciprocal(inverse[:], unit[:])
+        window = [near, far]
 
-        nc.gpsimd.tensor_scalar(grouped[1][:, 0], w_far[0][:].rearrange("p t m -> p m t"), 1.0, 0.0, MULT, ADD)
+        def values(name, entries, tag):
+            return keep.tile([P, entries.stop - entries.start], F32, name=name, tag=tag, align_bytes=64)
 
-        gate_opening = keep.tile([P, QUARTER], F32, name="gate_opening", tag="part_then_gate", align_bytes=64)
-        make_gate(gate_opening[:], acc[0][0][:, opening])
-        nc.scalar.copy(grouped[1][:, 1], w_far[1][:].rearrange("p t m -> p m t"))
-        gate_second = far_pool.tile([P, HALF], F32, name="gate_second", offset=far_bytes + pass_bytes // 2, align_bytes=64)
-        make_gate(gate_second[:], acc[0][1][:])
-        put(near, opening, old_near[:, opening], gate_opening[:])
-        quantize(1)
-        for h, entries in enumerate((first, second)):
-            for z in range(PASSES):
-                multiply(acc[1][h], 1, z, entries)
-        put(near, second, old_near[:, second], gate_second[:])
+        def make_gate(gate, b, entries):
+            h = entries.start // 512
+            nc.scalar.activation(gate, acc[b][h][:, entries.start - 512 * h : entries.stop - 512 * h], ACT.Sigmoid)
 
-        scaled = far_pool.tile([P, U], F32, name="scaled", offset=far_bytes + 3 * pass_bytes // 2, align_bytes=64)
-        nc.scalar.activation(scaled[:], far[:], ACT.Copy, scale=inverse[:])
+        def fetch_vector(old, b, entries):
+            nc.vector.tensor_copy(old, window[b][:].indirect(slot_sb[:, columns(entries)]))
 
-        gate_far = keep.tile([P, S], F32, name="gate_far", align_bytes=64)
-        make_gate(gate_far[:, first], acc[1][0][:])
-        put(far, by_vector, old_far[:], gate_far[:, by_vector])
+        def product(new, old, gate):
+            nc.gpsimd.tensor_tensor(new, old, gate, MULT)
 
-        raised = keep.tile([P, S - SHARE], F32, name="raised", align_bytes=64)
-        nc.scalar.activation(raised[:], scaled[:].indirect(slot_sb[:, columns(by_scalar)]), ACT.Sigmoid, bias=-SHIFT)
-        make_gate(gate_far[:, second], acc[1][1][:])
+        def put_scalar(b, entries, new):
+            nc.scalar.activation(window[b][:].indirect(slot_sb[:, columns(entries)]), new, ACT.Copy)
 
-        gate_closing = keep.tile([P, QUARTER], F32, name="gate_closing", tag="inverse_then_gate", align_bytes=64)
-        make_gate(gate_closing[:], acc[0][0][:, closing])
-        put(near, closing, old_near[:, closing], gate_closing[:])
+        first, second = halves
+        gate = [values(f"gate{b}", slice(0, S), f"gate{b}") for b in range(2)]
+        for entries in halves:
+            for b in range(2):
+                make_gate(gate[b][:, entries], b, entries)
+        pieces = (slice(0, 256), slice(256, 640), slice(640, 1024))
+        old_near = values("old_near", slice(0, S), "old_near")
+        for entries in (slice(0, 256), slice(256, 1024)):
+            fetch_vector(old_near[:, entries], 0, entries)
+        new_near = values("new_near", slice(0, S), "new_near")
+        for entries in pieces:
+            product(new_near[:, entries], old_near[:, entries], gate[0][:, entries])
+            put_scalar(0, entries, new_near[:, entries])
         nc.sync.dma_start(out[0:P, :], near[:])
-
-        gate_unit = keep.tile([P, S - SHARE], F32, name="gate_unit", align_bytes=64)
-        nc.scalar.activation(gate_unit[:], gate_far[:, by_scalar], ACT.Copy, scale=unit[:])
-        lowered = keep.tile([P, S - SHARE], F32, name="lowered", align_bytes=64)
-        nc.scalar.activation(lowered[:], raised[:], ACT.Ln, scale=math.exp(SHIFT))
-        put(far, by_scalar, lowered[:], gate_unit[:])
+        old_far = values("old_far", slice(0, S), "old_far")
+        fetch_vector(old_far[:], 1, slice(0, S))
+        nc.vector.tensor_tensor(far[:].indirect(slot_sb[:]), old_far[:], gate[1][:], MULT)
         nc.sync.dma_start(out[P : 2 * P, :], far[:])

@@ -32,6 +32,7 @@ def tile_picked_idxput_gate_p_kernel(tc, x_words, x_scales, mem, w1, offs, slot,
     with ExitStack() as ctx:
         keep = ctx.enter_context(tc.tile_pool(name="keep", bufs=1))
         rows_pool = ctx.enter_context(tc.tile_pool(name="rows_pool", bufs=1))
+        late_pool = ctx.enter_context(tc.tile_pool(name="late_pool", bufs=1))
         psum = ctx.enter_context(tc.psum_pool(name="psum", bufs=1))
 
         def columns(entries):
@@ -42,10 +43,10 @@ def tile_picked_idxput_gate_p_kernel(tc, x_words, x_scales, mem, w1, offs, slot,
         row_bytes = 4 * U
         scale_table = rows_pool.tile([P, T], U8, name="scale_table", offset=row_bytes - T // 2, align_bytes=64)
         word_table = [
-            keep.tile([P, 4 * S], U16, name="word_table0", align_bytes=64),
+            keep.tile([P, 3 * S], U16, name="word_table0", align_bytes=64),
             keep.tile([P, T], U16, name="word_table1", align_bytes=64),
         ]
-        picked_scales = keep.tile([P, S], U8, name="picked_scales", align_bytes=64)
+        picked_scales = late_pool.tile([P, S], U8, name="picked_scales", offset=1024 - 64, align_bytes=64)
         x_scale = keep.tile([P, PASSES * S], U8, name="x_scale", align_bytes=64)
         nc.vector.memset(scale_table[0:TABLE_START, :].bitcast(I32), 0)
         nc.vector.memset(x_scale[:].bitcast(I32), 0)
@@ -72,10 +73,16 @@ def tile_picked_idxput_gate_p_kernel(tc, x_words, x_scales, mem, w1, offs, slot,
         nc.sync.dma_start(near[:], mem[0:P, :])
         nc.sync.dma_start(far[:], mem[P : 2 * P, :])
 
-        picked_words = [keep.tile([P, S], U16, name="picked_words0", align_bytes=64)]
-        nc.vector.tensor_copy(picked_words[0][:], word_table[0][:].indirect(offs_sb[:]))
+        early, late = slice(0, 640), slice(640, S)
 
-        grouped = [keep.tile([P, PASSES, P, PACK], BF16, name=f"grouped{b}", align_bytes=64) for b in range(2)]
+        def pick_words(z, entries, pool, offset=None):
+            words = pool.tile([P, entries.stop - entries.start], U16, name=f"words{z}_{entries.start}", offset=offset, align_bytes=64)
+            nc.vector.tensor_copy(words[:], word_table[z][:].indirect(offs_sb[:, columns(entries)]))
+            return words
+
+        words0_early = pick_words(0, early, keep)
+
+        grouped = [keep.tile([P, PASSES, P, PACK], BF16, name=f"grouped{b}", tag=f"grouped{b}", align_bytes=64) for b in range(2)]
         warm = keep.tile([P, 1], F32, name="warm", align_bytes=64)
         nc.vector.memset(warm[:], 0.0)
         warmed = keep.tile([P, 1], F32, name="warmed", align_bytes=64)
@@ -86,40 +93,52 @@ def tile_picked_idxput_gate_p_kernel(tc, x_words, x_scales, mem, w1, offs, slot,
                 w_raw[z][:, :, b * P : (b + 1) * P].rearrange("p t (c i) -> p c t i", i=4),
             )
 
-        cast(0, 0)
-        nc.gpsimd.tensor_scalar(grouped[1][:, 0], w_raw[0][:, :, P:N].rearrange("p t m -> p m t"), 1.0, 0.0, MULT, ADD)
-        cast(0, 1)
-        cast(1, 1)
+        for z in range(PASSES):
+            cast(0, z)
+            nc.gpsimd.tensor_scalar(grouped[1][:, z], w_raw[z][:, :, P:N].rearrange("p t m -> p m t"), 1.0, 0.0, MULT, ADD)
         w_codes = [keep.tile([P, PASSES * P], U32, name=f"w_codes{b}", tag=f"w_codes{b}", align_bytes=64) for b in range(2)]
-        w_scale = [keep.tile([P, PASSES * P], U8, name=f"w_scale{b}", align_bytes=64) for b in range(2)]
-        for b in range(2):
+        w_scale = [
+            keep.tile([P, PASSES * P], U8, name="w_scale0", align_bytes=64),
+            late_pool.tile([P, PASSES * P], U8, name="w_scale1", offset=1024 + 256, align_bytes=64),
+        ]
+
+        def quantize(b):
             nc.vector.quantize_mx(w_codes[b][:].bitcast(FP8X4), w_scale[b][:], grouped[b][:].rearrange("p z m t -> p (z m t)"))
 
-        halves = (slice(0, 512), slice(512, 1024))
-        picked_late = []
-        for h, entries in enumerate(halves):
-            picked_late.append(keep.tile([P, 512], U16, name=f"picked_late{h}", tag=f"w_raw{1 - h}", align_bytes=64))
-            nc.vector.tensor_copy(picked_late[h][:], word_table[1][:].indirect(offs_sb[:, columns(entries)]))
+        first, second = slice(0, 512), slice(512, S)
+        quantize(0)
+        words1_first = pick_words(1, first, keep)
+        quantize(1)
+        words0_late = pick_words(0, late, late_pool, 1024 - 2 * 384)
+        words1_second = pick_words(1, second, late_pool, 2048 - 128)
 
-        def multiply(acc, b, h):
-            entries = halves[h]
-            for z, words in enumerate((picked_words[0][:, entries], picked_late[h][:])):
-                w_cols = slice(z * P, (z + 1) * P)
-                nc.tensor.matmul_mx(
-                    out=acc[:],
-                    lhsT=w_codes[b][:, w_cols].bitcast(FP8X4),
-                    lhsT_scale=w_scale[b][:, w_cols],
-                    rhs=words.bitcast(FP4X4),
-                    rhs_scale=x_scale[:, z * S + entries.start : z * S + entries.stop],
-                    start=(z == 0),
-                    stop=(z == PASSES - 1),
-                )
+        acc = [[psum.tile([P, 512], F32, name=f"acc0{h}") for h in range(2)], [psum.tile([P, 512], F32, name="acc10", tag="far_bank")]]
 
-        acc = [[psum.tile([P, 512], F32, name=f"acc{b}{h}") for h in range(2)] for b in range(2)]
-        for h in range(2):
-            for b in range(2):
-                multiply(acc[b][h], b, h)
+        def multiply(b, z, entries, words, start, stop):
+            h = entries.start // 512
+            w_cols = slice(z * P, (z + 1) * P)
+            nc.tensor.matmul_mx(
+                out=acc[b][h][:, entries.start - 512 * h : entries.stop - 512 * h],
+                lhsT=w_codes[b][:, w_cols].bitcast(FP8X4),
+                lhsT_scale=w_scale[b][:, w_cols],
+                rhs=words.bitcast(FP4X4),
+                rhs_scale=x_scale[:, z * S + entries.start : z * S + entries.stop],
+                start=start,
+                stop=stop,
+            )
 
+        multiply(0, 0, first, words0_early[:, first], True, False)
+        multiply(0, 1, first, words1_first[:], False, True)
+        multiply(1, 0, first, words0_early[:, first], True, False)
+        multiply(1, 1, first, words1_first[:], False, True)
+
+        def multiply_second(b):
+            multiply(b, 0, slice(512, 640), words0_early[:, 512:640], True, False)
+            multiply(b, 0, slice(640, 896), words0_late[:, 0:256], False, False)
+            multiply(b, 0, slice(896, 1024), words0_late[:, 256:384], False, False)
+            multiply(b, 1, second, words1_second[:], False, True)
+
+        multiply_second(0)
         window = [near, far]
 
         def values(name, entries, tag):
@@ -128,6 +147,9 @@ def tile_picked_idxput_gate_p_kernel(tc, x_words, x_scales, mem, w1, offs, slot,
         def make_gate(gate, b, entries):
             h = entries.start // 512
             nc.scalar.activation(gate, acc[b][h][:, entries.start - 512 * h : entries.stop - 512 * h], ACT.Sigmoid)
+
+        def fetch_scalar(old, b, entries):
+            nc.scalar.activation(old, window[b][:].indirect(slot_sb[:, columns(entries)]), ACT.Copy)
 
         def fetch_vector(old, b, entries):
             nc.vector.tensor_copy(old, window[b][:].indirect(slot_sb[:, columns(entries)]))
@@ -138,21 +160,32 @@ def tile_picked_idxput_gate_p_kernel(tc, x_words, x_scales, mem, w1, offs, slot,
         def put_scalar(b, entries, new):
             nc.scalar.activation(window[b][:].indirect(slot_sb[:, columns(entries)]), new, ACT.Copy)
 
-        first, second = halves
-        gate = [values(f"gate{b}", slice(0, S), f"gate{b}") for b in range(2)]
-        for entries in halves:
-            for b in range(2):
-                make_gate(gate[b][:, entries], b, entries)
+        gates = values("gates", slice(0, 2 * S + 384), "gates")
         pieces = (slice(0, 256), slice(256, 640), slice(640, 1024))
-        old_near = values("old_near", slice(0, S), "old_near")
-        for entries in (slice(0, 256), slice(256, 1024)):
-            fetch_vector(old_near[:, entries], 0, entries)
         new_near = values("new_near", slice(0, S), "new_near")
-        for entries in pieces:
-            product(new_near[:, entries], old_near[:, entries], gate[0][:, entries])
-            put_scalar(0, entries, new_near[:, entries])
-        nc.sync.dma_start(out[0:P, :], near[:])
         old_far = values("old_far", slice(0, S), "old_far")
+
+        make_gate(gates[:, first], 0, first)
+        fetch_scalar(gates[:, 896:1152], 0, slice(0, 256))
+        fetch_scalar(gates[:, 1536:1792], 0, slice(256, 512))
+        fetch_vector(gates[:, 1920:2432], 0, slice(512, 1024))
+        product(new_near[:, 128:256], gates[:, 1024:1152], gates[:, 128:256])
+        make_gate(gates[:, 1024:1536], 1, first)
+        acc[1].append(psum.tile([P, 512], F32, name="acc11", tag="far_bank"))
+        multiply_second(1)
+        product(new_near[:, 0:128], gates[:, 896:1024], gates[:, 0:128])
+        make_gate(gates[:, second], 0, second)
+        product(new_near[:, 256:512], gates[:, 1536:1792], gates[:, 256:512])
+        put_scalar(0, pieces[0], new_near[:, pieces[0]])
+        make_gate(gates[:, 1536:1792], 1, slice(512, 768))
+        product(new_near[:, 512:640], gates[:, 1920:2048], gates[:, 512:640])
+        put_scalar(0, pieces[1], new_near[:, pieces[1]])
+        make_gate(gates[:, 1792:2048], 1, slice(768, 1024))
+        product(new_near[:, 640:1024], gates[:, 2048:2432], gates[:, 640:1024])
+        put_scalar(0, pieces[2], new_near[:, pieces[2]])
+        nc.sync.dma_start(out[0:P, :], near[:])
         fetch_vector(old_far[:], 1, slice(0, S))
-        nc.vector.tensor_tensor(far[:].indirect(slot_sb[:]), old_far[:], gate[1][:], MULT)
+        for entries in (slice(0, 768), slice(768, S)):
+            gate = gates[:, S + entries.start : S + entries.stop]
+            nc.vector.tensor_tensor(far[:].indirect(slot_sb[:, columns(entries)]), old_far[:, entries], gate, MULT)
         nc.sync.dma_start(out[P : 2 * P, :], far[:])

@@ -87,19 +87,25 @@ def tile_picked_idxput_gate_p_kernel(tc, x_words, x_scales, mem, w1, offs, slot,
         nc.vector.memset(warm[:], 0.0)
         warmed = keep.tile([P, 1], F32, name="warmed", align_bytes=64)
         nc.scalar.activation(warmed[:], warm[:], ACT.Sigmoid)
-        def cast(b, z):
+        def cast_scalar(b, z, cols):
             nc.scalar.copy(
-                grouped[b][:, z].rearrange("p (c i) t -> p c t i", i=4),
-                w_raw[z][:, :, b * P : (b + 1) * P].rearrange("p t (c i) -> p c t i", i=4),
+                grouped[b][:, z, cols].rearrange("p (c i) t -> p c t i", i=4),
+                w_raw[z][:, :, b * P + cols.start : b * P + cols.stop].rearrange("p t (c i) -> p c t i", i=4),
             )
 
-        for z in range(PASSES):
-            cast(0, z)
-            nc.gpsimd.tensor_scalar(grouped[1][:, z], w_raw[z][:, :, P:N].rearrange("p t m -> p m t"), 1.0, 0.0, MULT, ADD)
+        def cast_gpsimd(b, z, cols):
+            raw = w_raw[z][:, :, b * P + cols.start : b * P + cols.stop]
+            nc.gpsimd.tensor_scalar(grouped[b][:, z, cols], raw.rearrange("p t m -> p m t"), 1.0, 0.0, MULT, ADD)
+
+        cast_scalar(0, 0, slice(0, P))
+        cast_gpsimd(1, 0, slice(0, P))
+        for b in range(2):
+            cast_scalar(b, 1, slice(0, 72))
+            cast_gpsimd(b, 1, slice(72, P))
         w_codes = [keep.tile([P, PASSES * P], U32, name=f"w_codes{b}", tag=f"w_codes{b}", align_bytes=64) for b in range(2)]
         w_scale = [
             keep.tile([P, PASSES * P], U8, name="w_scale0", align_bytes=64),
-            late_pool.tile([P, PASSES * P], U8, name="w_scale1", offset=1024 + 256, align_bytes=64),
+            keep.tile([P, PASSES * P], U8, name="w_scale1", align_bytes=64),
         ]
 
         def quantize(b):
@@ -107,46 +113,47 @@ def tile_picked_idxput_gate_p_kernel(tc, x_words, x_scales, mem, w1, offs, slot,
 
         first, second = slice(0, 512), slice(512, S)
         quantize(0)
-        words1_first = pick_words(1, first, keep)
         quantize(1)
+        quarters = [slice(a, a + 256) for a in range(0, S, 256)]
+        words1_first = keep.tile([P, 512], U16, name="words1_first", tag="w_raw1", align_bytes=64)
+        for entries in quarters[0:2]:
+            nc.vector.tensor_copy(words1_first[:, entries], word_table[1][:].indirect(offs_sb[:, columns(entries)]))
         words0_late = pick_words(0, late, late_pool, 1024 - 2 * 384)
-        words1_second = pick_words(1, second, late_pool, 2048 - 128)
+        words1_second = late_pool.tile([P, 512], U16, name="words1_second", offset=2048 - 128, align_bytes=64)
+        for h, entries in enumerate(quarters[2:4]):
+            nc.vector.tensor_copy(words1_second[:, quarters[h]], word_table[1][:].indirect(offs_sb[:, columns(entries)]))
 
-        acc = [[psum.tile([P, 512], F32, name=f"acc0{h}") for h in range(2)], [psum.tile([P, 512], F32, name="acc10", tag="far_bank")]]
+        def words(z, entries):
+            tile, start = ((words0_early, 0), (words0_late, late.start), (words1_first, 0), (words1_second, 512))[
+                2 * z + (entries.start >= (late.start, 512)[z])
+            ]
+            return tile[:, entries.start - start : entries.stop - start]
 
-        def multiply(b, z, entries, words, start, stop):
-            h = entries.start // 512
-            w_cols = slice(z * P, (z + 1) * P)
-            nc.tensor.matmul_mx(
-                out=acc[b][h][:, entries.start - 512 * h : entries.stop - 512 * h],
-                lhsT=w_codes[b][:, w_cols].bitcast(FP8X4),
-                lhsT_scale=w_scale[b][:, w_cols],
-                rhs=words.bitcast(FP4X4),
-                rhs_scale=x_scale[:, z * S + entries.start : z * S + entries.stop],
-                start=start,
-                stop=stop,
-            )
+        def multiply(acc, b, entries, cuts):
+            steps = [(0, slice(a, c)) for a, c in zip(cuts[:-1], cuts[1:])] + [(1, entries)]
+            for i, (z, part) in enumerate(steps):
+                w_cols = slice(z * P, (z + 1) * P)
+                nc.tensor.matmul_mx(
+                    out=acc[:, part.start - entries.start : part.stop - entries.start],
+                    lhsT=w_codes[b][:, w_cols].bitcast(FP8X4),
+                    lhsT_scale=w_scale[b][:, w_cols],
+                    rhs=words(z, part).bitcast(FP4X4),
+                    rhs_scale=x_scale[:, z * S + part.start : z * S + part.stop],
+                    start=(i == 0),
+                    stop=(i == len(steps) - 1),
+                )
 
-        multiply(0, 0, first, words0_early[:, first], True, False)
-        multiply(0, 1, first, words1_first[:], False, True)
-        multiply(1, 0, first, words0_early[:, first], True, False)
-        multiply(1, 1, first, words1_first[:], False, True)
-
-        def multiply_second(b):
-            multiply(b, 0, slice(512, 640), words0_early[:, 512:640], True, False)
-            multiply(b, 0, slice(640, 896), words0_late[:, 0:256], False, False)
-            multiply(b, 0, slice(896, 1024), words0_late[:, 256:384], False, False)
-            multiply(b, 1, second, words1_second[:], False, True)
-
-        multiply_second(0)
+        near_acc = [psum.tile([P, 512], F32, name=f"near_acc{i}") for i in range(4)]
+        far_acc = psum.tile([P, 512], F32, name="far_acc0", tag="far_bank")
+        multiply(near_acc[0], 0, quarters[0], (0, 256))
+        multiply(near_acc[1], 0, quarters[1], (256, 512))
+        multiply(far_acc, 1, first, (0, 512))
+        multiply(near_acc[2], 0, quarters[2], (512, 640, 768))
+        multiply(near_acc[3], 0, quarters[3], (768, 1024))
         window = [near, far]
 
-        def values(name, entries, tag):
-            return keep.tile([P, entries.stop - entries.start], F32, name=name, tag=tag, align_bytes=64)
-
-        def make_gate(gate, b, entries):
-            h = entries.start // 512
-            nc.scalar.activation(gate, acc[b][h][:, entries.start - 512 * h : entries.stop - 512 * h], ACT.Sigmoid)
+        def make_gate(gate, acc):
+            nc.scalar.activation(gate, acc, ACT.Sigmoid)
 
         def fetch_scalar(old, b, entries):
             nc.scalar.activation(old, window[b][:].indirect(slot_sb[:, columns(entries)]), ACT.Copy)
@@ -154,38 +161,40 @@ def tile_picked_idxput_gate_p_kernel(tc, x_words, x_scales, mem, w1, offs, slot,
         def fetch_vector(old, b, entries):
             nc.vector.tensor_copy(old, window[b][:].indirect(slot_sb[:, columns(entries)]))
 
-        def product(new, old, gate):
-            nc.gpsimd.tensor_tensor(new, old, gate, MULT)
+        def product(entries, old, gate):
+            nc.gpsimd.tensor_tensor(new_near[:, entries], old, gate, MULT)
 
-        def put_scalar(b, entries, new):
-            nc.scalar.activation(window[b][:].indirect(slot_sb[:, columns(entries)]), new, ACT.Copy)
+        def put_scalar(entries):
+            nc.scalar.activation(near[:].indirect(slot_sb[:, columns(entries)]), new_near[:, entries], ACT.Copy)
 
-        gates = values("gates", slice(0, 2 * S + 384), "gates")
-        pieces = (slice(0, 256), slice(256, 640), slice(640, 1024))
-        new_near = values("new_near", slice(0, S), "new_near")
-        old_far = values("old_far", slice(0, S), "old_far")
+        work = keep.tile([P, 1920], F32, name="work", align_bytes=64)
+        new_near = keep.tile([P, S], F32, name="new_near", align_bytes=64)
+        old_far = keep.tile([P, S], F32, name="old_far", align_bytes=64)
 
-        make_gate(gates[:, first], 0, first)
-        fetch_scalar(gates[:, 896:1152], 0, slice(0, 256))
-        fetch_scalar(gates[:, 1536:1792], 0, slice(256, 512))
-        fetch_vector(gates[:, 1920:2432], 0, slice(512, 1024))
-        product(new_near[:, 128:256], gates[:, 1024:1152], gates[:, 128:256])
-        make_gate(gates[:, 1024:1536], 1, first)
-        acc[1].append(psum.tile([P, 512], F32, name="acc11", tag="far_bank"))
-        multiply_second(1)
-        product(new_near[:, 0:128], gates[:, 896:1024], gates[:, 0:128])
-        make_gate(gates[:, second], 0, second)
-        product(new_near[:, 256:512], gates[:, 1536:1792], gates[:, 256:512])
-        put_scalar(0, pieces[0], new_near[:, pieces[0]])
-        make_gate(gates[:, 1536:1792], 1, slice(512, 768))
-        product(new_near[:, 512:640], gates[:, 1920:2048], gates[:, 512:640])
-        put_scalar(0, pieces[1], new_near[:, pieces[1]])
-        make_gate(gates[:, 1792:2048], 1, slice(768, 1024))
-        product(new_near[:, 640:1024], gates[:, 2048:2432], gates[:, 640:1024])
-        put_scalar(0, pieces[2], new_near[:, pieces[2]])
+        make_gate(work[:, 128:384], near_acc[0][:, 0:256])
+        make_gate(work[:, 1024:1280], near_acc[1][:, 0:256])
+        fetch_scalar(work[:, 512:640], 0, slice(0, 128))
+        fetch_scalar(new_near[:, 384:640], 0, slice(128, 384))
+        fetch_vector(work[:, 1280:1920], 0, slice(384, 1024))
+        product(slice(0, 128), work[:, 512:640], work[:, 128:256])
+        make_gate(work[:, 512:1024], far_acc[:])
+        far_acc = psum.tile([P, 512], F32, name="far_acc1", tag="far_bank")
+        multiply(far_acc, 1, second, (512, 640, 896, 1024))
+        make_gate(work[:, 0:256], near_acc[2][:, 0:256])
+        product(slice(128, 256), new_near[:, 384:512], work[:, 256:384])
+        make_gate(work[:, 256:512], near_acc[3][:, 0:256])
+        product(slice(256, 384), new_near[:, 512:640], work[:, 1024:1152])
+        put_scalar(slice(0, 256))
+        product(slice(384, 512), work[:, 1280:1408], work[:, 1152:1280])
+        make_gate(work[:, 1024:1280], far_acc[:, 0:256])
+        product(slice(512, 640), work[:, 1408:1536], work[:, 0:128])
+        put_scalar(slice(256, 640))
+        make_gate(work[:, 1280:1536], far_acc[:, 256:512])
+        product(slice(640, 1024), work[:, 1536:1920], work[:, 128:512])
+        put_scalar(slice(640, 1024))
         nc.sync.dma_start(out[0:P, :], near[:])
         fetch_vector(old_far[:], 1, slice(0, S))
         for entries in (slice(0, 768), slice(768, S)):
-            gate = gates[:, S + entries.start : S + entries.stop]
+            gate = work[:, 512 + entries.start : 512 + entries.stop]
             nc.vector.tensor_tensor(far[:].indirect(slot_sb[:, columns(entries)]), old_far[:, entries], gate, MULT)
         nc.sync.dma_start(out[P : 2 * P, :], far[:])

@@ -43,7 +43,7 @@ def tile_picked_idxput_gate_p_kernel(tc, x_words, x_scales, mem, w1, offs, slot,
         row_bytes = 4 * U
         scale_table = rows_pool.tile([P, T], U8, name="scale_table", offset=row_bytes - T // 2, align_bytes=64)
         word_table = [
-            keep.tile([P, 3 * S], U16, name="word_table0", align_bytes=64),
+            keep.tile([P, 4 * S], U16, name="word_table0", align_bytes=64),
             keep.tile([P, T], U16, name="word_table1", align_bytes=64),
         ]
         picked_scales = late_pool.tile([P, S], U8, name="picked_scales", offset=1024 - 64, align_bytes=64)
@@ -73,35 +73,25 @@ def tile_picked_idxput_gate_p_kernel(tc, x_words, x_scales, mem, w1, offs, slot,
         nc.sync.dma_start(near[:], mem[0:P, :])
         nc.sync.dma_start(far[:], mem[P : 2 * P, :])
 
-        early, late = slice(0, 640), slice(640, S)
-
-        def pick_words(z, entries, pool, offset=None):
-            words = pool.tile([P, entries.stop - entries.start], U16, name=f"words{z}_{entries.start}", offset=offset, align_bytes=64)
-            nc.vector.tensor_copy(words[:], word_table[z][:].indirect(offs_sb[:, columns(entries)]))
-            return words
-
-        words0_early = pick_words(0, early, keep)
+        words0 = keep.tile([P, S], U16, name="words0", align_bytes=64)
+        nc.vector.tensor_copy(words0[:], word_table[0][:].indirect(offs_sb[:]))
 
         grouped = [keep.tile([P, PASSES, P, PACK], BF16, name=f"grouped{b}", tag=f"grouped{b}", align_bytes=64) for b in range(2)]
         warm = keep.tile([P, 1], F32, name="warm", align_bytes=64)
         nc.vector.memset(warm[:], 0.0)
         warmed = keep.tile([P, 1], F32, name="warmed", align_bytes=64)
         nc.scalar.activation(warmed[:], warm[:], ACT.Sigmoid)
-        def cast_scalar(b, z, cols):
+
+        def cast(b, z):
             nc.scalar.copy(
-                grouped[b][:, z, cols].rearrange("p (c i) t -> p c t i", i=4),
-                w_raw[z][:, :, b * P + cols.start : b * P + cols.stop].rearrange("p t (c i) -> p c t i", i=4),
+                grouped[b][:, z].rearrange("p (c i) t -> p c t i", i=4),
+                w_raw[z][:, :, b * P : (b + 1) * P].rearrange("p t (c i) -> p c t i", i=4),
             )
 
-        def cast_gpsimd(b, z, cols):
-            raw = w_raw[z][:, :, b * P + cols.start : b * P + cols.stop]
-            nc.gpsimd.tensor_scalar(grouped[b][:, z, cols], raw.rearrange("p t m -> p m t"), 1.0, 0.0, MULT, ADD)
-
-        cast_scalar(0, 0, slice(0, P))
-        cast_gpsimd(1, 0, slice(0, P))
-        for b in range(2):
-            cast_scalar(b, 1, slice(0, 72))
-            cast_gpsimd(b, 1, slice(72, P))
+        cast(0, 0)
+        nc.gpsimd.tensor_scalar(grouped[1][:, 0], w_raw[0][:, :, P:N].rearrange("p t m -> p m t"), 1.0, 0.0, MULT, ADD)
+        cast(0, 1)
+        cast(1, 1)
         w_codes = [keep.tile([P, PASSES * P], U32, name=f"w_codes{b}", tag=f"w_codes{b}", align_bytes=64) for b in range(2)]
         w_scale = [
             keep.tile([P, PASSES * P], U8, name="w_scale0", align_bytes=64),
@@ -113,21 +103,21 @@ def tile_picked_idxput_gate_p_kernel(tc, x_words, x_scales, mem, w1, offs, slot,
 
         first, second = slice(0, 512), slice(512, S)
         quantize(0)
-        quantize(1)
         quarters = [slice(a, a + 256) for a in range(0, S, 256)]
-        words1_first = keep.tile([P, 512], U16, name="words1_first", tag="w_raw1", align_bytes=64)
+        words1_first = keep.tile([P, 512], U16, name="words1_first", align_bytes=64)
         for entries in quarters[0:2]:
             nc.vector.tensor_copy(words1_first[:, entries], word_table[1][:].indirect(offs_sb[:, columns(entries)]))
-        words0_late = pick_words(0, late, late_pool, 1024 - 2 * 384)
+        quantize(1)
         words1_second = late_pool.tile([P, 512], U16, name="words1_second", offset=2048 - 128, align_bytes=64)
         for h, entries in enumerate(quarters[2:4]):
             nc.vector.tensor_copy(words1_second[:, quarters[h]], word_table[1][:].indirect(offs_sb[:, columns(entries)]))
 
         def words(z, entries):
-            tile, start = ((words0_early, 0), (words0_late, late.start), (words1_first, 0), (words1_second, 512))[
-                2 * z + (entries.start >= (late.start, 512)[z])
-            ]
-            return tile[:, entries.start - start : entries.stop - start]
+            if z == 0:
+                return words0[:, entries]
+            if entries.start < 512:
+                return words1_first[:, entries]
+            return words1_second[:, entries.start - 512 : entries.stop - 512]
 
         def multiply(acc, b, entries, cuts):
             steps = [(0, slice(a, c)) for a, c in zip(cuts[:-1], cuts[1:])] + [(1, entries)]
@@ -148,7 +138,7 @@ def tile_picked_idxput_gate_p_kernel(tc, x_words, x_scales, mem, w1, offs, slot,
         multiply(near_acc[0], 0, quarters[0], (0, 256))
         multiply(near_acc[1], 0, quarters[1], (256, 512))
         multiply(far_acc, 1, first, (0, 512))
-        multiply(near_acc[2], 0, quarters[2], (512, 640, 768))
+        multiply(near_acc[2], 0, quarters[2], (512, 768))
         multiply(near_acc[3], 0, quarters[3], (768, 1024))
         window = [near, far]
 
@@ -179,7 +169,7 @@ def tile_picked_idxput_gate_p_kernel(tc, x_words, x_scales, mem, w1, offs, slot,
         product(slice(0, 128), work[:, 512:640], work[:, 128:256])
         make_gate(work[:, 512:1024], far_acc[:])
         far_acc = psum.tile([P, 512], F32, name="far_acc1", tag="far_bank")
-        multiply(far_acc, 1, second, (512, 640, 896, 1024))
+        multiply(far_acc, 1, second, (512, 1024))
         make_gate(work[:, 0:256], near_acc[2][:, 0:256])
         product(slice(128, 256), new_near[:, 384:512], work[:, 256:384])
         make_gate(work[:, 256:512], near_acc[3][:, 0:256])

@@ -61,7 +61,7 @@ def tile_picked_idxput_gate_p_kernel(tc, x_words, x_scales, mem, w1, offs, slot,
         nc.sync.dma_start(slot_sb[:], slot)
 
         nc.vector.tensor_copy(picked_scales[:], scale_table[:].indirect(offs_sb[:]))
-        for q in range(QUADRANTS):
+        for q in (0, 2, 1, 3):
             start = TABLE_START + q * SCALE_ROWS * PASSES
             rows = x_scale[q * QUADRANT : q * QUADRANT + SCALE_ROWS, :]
             nc.sync.dma_start(

@@ -50,6 +50,8 @@ def tile_picked_idxput_gate_p_kernel(tc, x_words, x_scales, mem, w1, offs, slot,
         x_scale = keep.tile([P, PASSES * S], U8, name="x_scale", align_bytes=64)
         nc.vector.memset(scale_table[0:TABLE_START, :].bitcast(I32), 0)
         nc.vector.memset(x_scale[:].bitcast(I32), 0)
+        ones = keep.tile([P, 1], F32, name="ones", align_bytes=64)
+        nc.vector.memset(ones[:], 1.0)
 
         w_raw = [keep.tile([P, PACK, N], F32, name=f"w_raw{z}", tag=f"w_raw{z}", align_bytes=64) for z in range(PASSES)]
         nc.sync.dma_start(scale_table[TABLE_START:P, :].bitcast(I32), x_scales.rearrange("z i c -> i z c").bitcast(I32))
@@ -109,8 +111,7 @@ def tile_picked_idxput_gate_p_kernel(tc, x_words, x_scales, mem, w1, offs, slot,
             nc.vector.tensor_copy(words1_first[:, entries], word_table[1][:].indirect(offs_sb[:, columns(entries)]))
         quantize(1)
         words1_second = late_pool.tile([P, 512], U16, name="words1_second", offset=2048 - 128, align_bytes=64)
-        for h, entries in enumerate(quarters[2:4]):
-            nc.vector.tensor_copy(words1_second[:, quarters[h]], word_table[1][:].indirect(offs_sb[:, columns(entries)]))
+        nc.vector.tensor_copy(words1_second[:], word_table[1][:].indirect(offs_sb[:, columns(second)]))
 
         def words(z, entries):
             if z == 0:
@@ -133,13 +134,12 @@ def tile_picked_idxput_gate_p_kernel(tc, x_words, x_scales, mem, w1, offs, slot,
                     stop=(i == len(steps) - 1),
                 )
 
-        near_acc = [psum.tile([P, 512], F32, name=f"near_acc{i}") for i in range(4)]
+        near_acc = [psum.tile([P, 512], F32, name=f"near_acc{i}") for i in range(3)]
         far_acc = psum.tile([P, 512], F32, name="far_acc0", tag="far_bank")
         multiply(near_acc[0], 0, quarters[0], (0, 256))
         multiply(near_acc[1], 0, quarters[1], (256, 512))
         multiply(far_acc, 1, first, (0, 512))
-        multiply(near_acc[2], 0, quarters[2], (512, 768))
-        multiply(near_acc[3], 0, quarters[3], (768, 1024))
+        multiply(near_acc[2], 0, second, (512, 1024))
         window = [near, far]
 
         def make_gate(gate, acc):
@@ -155,36 +155,34 @@ def tile_picked_idxput_gate_p_kernel(tc, x_words, x_scales, mem, w1, offs, slot,
             nc.gpsimd.tensor_tensor(new_near[:, entries], old, gate, MULT)
 
         def put_scalar(entries):
-            nc.scalar.activation(near[:].indirect(slot_sb[:, columns(entries)]), new_near[:, entries], ACT.Copy)
+            nc.scalar.activation(near[:].indirect(slot_sb[:, columns(entries)]), new_near[:, entries], ACT.Copy, scale=ones[:])
 
-        work = keep.tile([P, 1920], F32, name="work", align_bytes=64)
+        LEAD = 64
+        SHARE = 320
+        FAR = 1024 - LEAD
+        OLD = FAR + S - 256
+        G0 = 768 - LEAD
+        work = keep.tile([P, OLD + S], F32, name="work", align_bytes=64)
         new_near = keep.tile([P, S], F32, name="new_near", align_bytes=64)
         old_far = keep.tile([P, S], F32, name="old_far", align_bytes=64)
 
-        make_gate(work[:, 128:384], near_acc[0][:, 0:256])
-        make_gate(work[:, 1024:1280], near_acc[1][:, 0:256])
-        fetch_scalar(work[:, 512:640], 0, slice(0, 128))
-        fetch_scalar(new_near[:, 384:640], 0, slice(128, 384))
-        fetch_vector(work[:, 1280:1920], 0, slice(384, 1024))
-        product(slice(0, 128), work[:, 512:640], work[:, 128:256])
-        make_gate(work[:, 512:1024], far_acc[:])
+        make_gate(work[:, G0 : G0 + 256], near_acc[0][:, 0:256])
+        make_gate(work[:, 0:256], near_acc[1][:, 0:256])
+        fetch_scalar(work[:, FAR : FAR + LEAD], 0, slice(0, LEAD))
+        fetch_scalar(work[:, OLD + LEAD : OLD + SHARE], 0, slice(LEAD, SHARE))
+        fetch_vector(work[:, OLD + SHARE : OLD + S], 0, slice(SHARE, S))
+        product(slice(0, LEAD), work[:, FAR : FAR + LEAD], work[:, G0 : G0 + LEAD])
+        make_gate(work[:, FAR : FAR + 512], far_acc[:])
         far_acc = psum.tile([P, 512], F32, name="far_acc1", tag="far_bank")
         multiply(far_acc, 1, second, (512, 1024))
-        make_gate(work[:, 0:256], near_acc[2][:, 0:256])
-        product(slice(128, 256), new_near[:, 384:512], work[:, 256:384])
-        make_gate(work[:, 256:512], near_acc[3][:, 0:256])
-        product(slice(256, 384), new_near[:, 512:640], work[:, 1024:1152])
+        make_gate(work[:, 256:768], near_acc[2][:])
+        product(slice(LEAD, 256), work[:, OLD + LEAD : OLD + 256], work[:, G0 + LEAD : G0 + 256])
+        product(slice(256, SHARE), work[:, OLD + 256 : OLD + SHARE], work[:, 0 : SHARE - 256])
         put_scalar(slice(0, 256))
-        product(slice(384, 512), work[:, 1280:1408], work[:, 1152:1280])
-        make_gate(work[:, 1024:1280], far_acc[:, 0:256])
-        product(slice(512, 640), work[:, 1408:1536], work[:, 0:128])
-        put_scalar(slice(256, 640))
-        make_gate(work[:, 1280:1536], far_acc[:, 256:512])
-        product(slice(640, 1024), work[:, 1536:1920], work[:, 128:512])
-        put_scalar(slice(640, 1024))
+        product(slice(SHARE, S), work[:, OLD + SHARE : OLD + S], work[:, SHARE - 256 : 768])
+        make_gate(work[:, FAR + 512 : FAR + S], far_acc[:])
+        put_scalar(slice(256, S))
         nc.sync.dma_start(out[0:P, :], near[:])
         fetch_vector(old_far[:], 1, slice(0, S))
-        for entries in (slice(0, 768), slice(768, S)):
-            gate = work[:, 512 + entries.start : 512 + entries.stop]
-            nc.vector.tensor_tensor(far[:].indirect(slot_sb[:, columns(entries)]), old_far[:, entries], gate, MULT)
+        nc.vector.tensor_tensor(far[:].indirect(slot_sb[:]), old_far[:], work[:, FAR : FAR + S], MULT)
         nc.sync.dma_start(out[P : 2 * P, :], far[:])

@@ -41,19 +41,19 @@ def tile_picked_idxput_gate_p_kernel(tc, x_words, x_scales, mem, w1, offs, slot,
         offs_sb = keep.tile([P, S // 16], U16, name="offs_sb")
         slot_sb = keep.tile([P, S // 16], U16, name="slot_sb")
         row_bytes = 4 * U
-        scale_table = rows_pool.tile([P, T], U8, name="scale_table", offset=row_bytes - T // 2, align_bytes=64)
+        scale_table = rows_pool.tile([P, T], U8, name="scale_table", offset=row_bytes - T // 2, align_bytes=256)
         word_table = [
-            keep.tile([P, 4 * S], U16, name="word_table0", align_bytes=64),
-            keep.tile([P, T], U16, name="word_table1", align_bytes=64),
+            keep.tile([P, 4 * S], U16, name="word_table0", align_bytes=256),
+            keep.tile([P, T], U16, name="word_table1", align_bytes=256),
         ]
-        picked_scales = late_pool.tile([P, S], U8, name="picked_scales", offset=1024 - 64, align_bytes=64)
-        x_scale = keep.tile([P, PASSES * S], U8, name="x_scale", align_bytes=64)
+        picked_scales = late_pool.tile([P, S], U8, name="picked_scales", offset=0, align_bytes=256)
+        x_scale = keep.tile([P, PASSES * S], U8, name="x_scale", align_bytes=256)
         nc.vector.memset(scale_table[0:TABLE_START, :].bitcast(I32), 0)
         nc.vector.memset(x_scale[:].bitcast(I32), 0)
         ones = keep.tile([P, 1], F32, name="ones", align_bytes=64)
         nc.vector.memset(ones[:], 1.0)
 
-        w_raw = [keep.tile([P, PACK, N], F32, name=f"w_raw{z}", tag=f"w_raw{z}", align_bytes=64) for z in range(PASSES)]
+        w_raw = [keep.tile([P, PACK, N], F32, name=f"w_raw{z}", tag=f"w_raw{z}", align_bytes=256) for z in range(PASSES)]
         nc.sync.dma_start(scale_table[TABLE_START:P, :].bitcast(I32), x_scales.rearrange("z i c -> i z c").bitcast(I32))
         nc.sync.dma_start(offs_sb[:], offs)
         nc.sync.dma_start(word_table[0][:, 0:T].bitcast(I32), x_words[0].bitcast(I32))
@@ -70,8 +70,8 @@ def tile_picked_idxput_gate_p_kernel(tc, x_words, x_scales, mem, w1, offs, slot,
                 rows.rearrange("r (z c) -> r z c", z=PASSES).bitcast(I32),
                 picked_scales[start : start + SCALE_ROWS * PASSES, :].bitcast(I32),
             )
-        near = rows_pool.tile([P, U], F32, name="near", offset=0, align_bytes=64)
-        far = rows_pool.tile([P, U], F32, name="far", offset=row_bytes, align_bytes=64)
+        near = rows_pool.tile([P, U], F32, name="near", offset=0, align_bytes=256)
+        far = rows_pool.tile([P, U], F32, name="far", offset=row_bytes, align_bytes=256)
         nc.sync.dma_start(near[:], mem[0:P, :])
         nc.sync.dma_start(far[:], mem[P : 2 * P, :])
 
@@ -110,7 +110,7 @@ def tile_picked_idxput_gate_p_kernel(tc, x_words, x_scales, mem, w1, offs, slot,
         for entries in quarters[0:2]:
             nc.vector.tensor_copy(words1_first[:, entries], word_table[1][:].indirect(offs_sb[:, columns(entries)]))
         quantize(1)
-        words1_second = late_pool.tile([P, 512], U16, name="words1_second", offset=2048 - 128, align_bytes=64)
+        words1_second = late_pool.tile([P, 512], U16, name="words1_second", offset=768, align_bytes=256)
         nc.vector.tensor_copy(words1_second[:], word_table[1][:].indirect(offs_sb[:, columns(second)]))
 
         def words(z, entries):

@@ -120,26 +120,26 @@ def tile_picked_idxput_gate_p_kernel(tc, x_words, x_scales, mem, w1, offs, slot,
                 return words1_first[:, entries]
             return words1_second[:, entries.start - 512 : entries.stop - 512]
 
-        def multiply(acc, b, entries, cuts):
-            steps = [(0, slice(a, c)) for a, c in zip(cuts[:-1], cuts[1:])] + [(1, entries)]
-            for i, (z, part) in enumerate(steps):
+        def multiply(acc, b, entries, order):
+            for z in order:
                 w_cols = slice(z * P, (z + 1) * P)
                 nc.tensor.matmul_mx(
-                    out=acc[:, part.start - entries.start : part.stop - entries.start],
+                    out=acc[:, 0 : entries.stop - entries.start],
                     lhsT=w_codes[b][:, w_cols].bitcast(FP8X4),
                     lhsT_scale=w_scale[b][:, w_cols],
-                    rhs=words(z, part).bitcast(FP4X4),
-                    rhs_scale=x_scale[:, z * S + part.start : z * S + part.stop],
-                    start=(i == 0),
-                    stop=(i == len(steps) - 1),
+                    rhs=words(z, entries).bitcast(FP4X4),
+                    rhs_scale=x_scale[:, z * S + entries.start : z * S + entries.stop],
+                    start=(z == order[0]),
+                    stop=(z == order[-1]),
                 )
 
-        near_acc = [psum.tile([P, 512], F32, name=f"near_acc{i}") for i in range(3)]
+        near_acc = [psum.tile([P, 512], F32, name=f"near_acc{i}") for i in range(4)]
         far_acc = psum.tile([P, 512], F32, name="far_acc0", tag="far_bank")
-        multiply(near_acc[0], 0, quarters[0], (0, 256))
-        multiply(near_acc[1], 0, quarters[1], (256, 512))
-        multiply(far_acc, 1, first, (0, 512))
-        multiply(near_acc[2], 0, second, (512, 1024))
+        multiply(near_acc[0], 0, quarters[0], (0, 1))
+        multiply(near_acc[1], 0, quarters[1], (0, 1))
+        multiply(far_acc, 1, first, (0, 1))
+        multiply(near_acc[2], 0, quarters[2], (0, 1))
+        multiply(near_acc[3], 0, quarters[3], (1, 0))
         window = [near, far]
 
         def make_gate(gate, acc):
@@ -159,9 +159,9 @@ def tile_picked_idxput_gate_p_kernel(tc, x_words, x_scales, mem, w1, offs, slot,
 
         LEAD = 64
         SHARE = 320
-        FAR = 1024 - LEAD
+        FAR = 768
         OLD = FAR + S - 256
-        G0 = 768 - LEAD
+        G0 = 512 - LEAD
         work = keep.tile([P, OLD + S], F32, name="work", align_bytes=64)
         new_near = keep.tile([P, S], F32, name="new_near", align_bytes=64)
         old_far = keep.tile([P, S], F32, name="old_far", align_bytes=64)
@@ -174,9 +174,10 @@ def tile_picked_idxput_gate_p_kernel(tc, x_words, x_scales, mem, w1, offs, slot,
         product(slice(0, LEAD), work[:, FAR : FAR + LEAD], work[:, G0 : G0 + LEAD])
         make_gate(work[:, FAR : FAR + 512], far_acc[:])
         far_acc = psum.tile([P, 512], F32, name="far_acc1", tag="far_bank")
-        multiply(far_acc, 1, second, (512, 1024))
-        make_gate(work[:, 256:768], near_acc[2][:])
+        multiply(far_acc, 1, second, (0, 1))
+        make_gate(work[:, 256:512], near_acc[2][:, 0:256])
         product(slice(LEAD, 256), work[:, OLD + LEAD : OLD + 256], work[:, G0 + LEAD : G0 + 256])
+        make_gate(work[:, 512:768], near_acc[3][:, 0:256])
         product(slice(256, SHARE), work[:, OLD + 256 : OLD + SHARE], work[:, 0 : SHARE - 256])
         put_scalar(slice(0, 256))
         product(slice(SHARE, S), work[:, OLD + SHARE : OLD + S], work[:, SHARE - 256 : 768])

@@ -120,26 +120,31 @@ def tile_picked_idxput_gate_p_kernel(tc, x_words, x_scales, mem, w1, offs, slot,
                 return words1_first[:, entries]
             return words1_second[:, entries.start - 512 : entries.stop - 512]
 
-        def multiply(acc, b, entries, order):
-            for z in order:
+        def multiply(acc, b, parts, order):
+            steps = [(z, part) for z in order for part in parts]
+            for i, (z, part) in enumerate(steps):
                 w_cols = slice(z * P, (z + 1) * P)
                 nc.tensor.matmul_mx(
-                    out=acc[:, 0 : entries.stop - entries.start],
+                    out=acc[:, part.start - parts[0].start : part.stop - parts[0].start],
                     lhsT=w_codes[b][:, w_cols].bitcast(FP8X4),
                     lhsT_scale=w_scale[b][:, w_cols],
-                    rhs=words(z, entries).bitcast(FP4X4),
-                    rhs_scale=x_scale[:, z * S + entries.start : z * S + entries.stop],
-                    start=(z == order[0]),
-                    stop=(z == order[-1]),
+                    rhs=words(z, part).bitcast(FP4X4),
+                    rhs_scale=x_scale[:, z * S + part.start : z * S + part.stop],
+                    start=(i == 0),
+                    stop=(i == len(steps) - 1),
                 )
 
         near_acc = [psum.tile([P, 512], F32, name=f"near_acc{i}") for i in range(4)]
         far_acc = psum.tile([P, 512], F32, name="far_acc0", tag="far_bank")
-        multiply(near_acc[0], 0, quarters[0], (0, 1))
-        multiply(near_acc[1], 0, quarters[1], (0, 1))
-        multiply(far_acc, 1, first, (0, 1))
-        multiply(near_acc[2], 0, quarters[2], (0, 1))
-        multiply(near_acc[3], 0, quarters[3], (1, 0))
+        multiply(near_acc[0], 0, [quarters[0]], (0, 1))
+        multiply(near_acc[1], 0, [quarters[1]], (0, 1))
+        multiply(far_acc, 1, [quarters[0]], (0, 1))
+        next_acc = psum.tile([P, 512], F32, name="next_acc")
+        multiply(next_acc, 1, [quarters[1]], (0, 1))
+        multiply(near_acc[2], 0, [quarters[2]], (0, 1))
+        multiply(near_acc[3], 0, [quarters[3]], (1, 0))
+        early_acc = psum.tile([P, 512], F32, name="early_acc")
+        multiply(early_acc, 1, [slice(512, 640)], (0, 1))
         window = [near, far]
 
         def make_gate(gate, acc):
@@ -161,6 +166,7 @@ def tile_picked_idxput_gate_p_kernel(tc, x_words, x_scales, mem, w1, offs, slot,
         SHARE = 320
         FAR = 768
         OLD = FAR + S - 256
+        MID = FAR + 544 - LEAD
         G0 = 512 - LEAD
         work = keep.tile([P, OLD + S], F32, name="work", align_bytes=64)
         new_near = keep.tile([P, S], F32, name="new_near", align_bytes=64)
@@ -168,20 +174,23 @@ def tile_picked_idxput_gate_p_kernel(tc, x_words, x_scales, mem, w1, offs, slot,
 
         make_gate(work[:, G0 : G0 + 256], near_acc[0][:, 0:256])
         make_gate(work[:, 0:256], near_acc[1][:, 0:256])
-        fetch_scalar(work[:, FAR : FAR + LEAD], 0, slice(0, LEAD))
-        fetch_scalar(work[:, OLD + LEAD : OLD + SHARE], 0, slice(LEAD, SHARE))
+        fetch_scalar(work[:, FAR + 224 : FAR + 288], 0, slice(0, LEAD))
+        fetch_scalar(work[:, MID + LEAD : MID + 256], 0, slice(LEAD, 256))
+        fetch_scalar(work[:, OLD + 256 : OLD + SHARE], 0, slice(256, SHARE))
         fetch_vector(work[:, OLD + SHARE : OLD + S], 0, slice(SHARE, S))
-        product(slice(0, LEAD), work[:, FAR : FAR + LEAD], work[:, G0 : G0 + LEAD])
-        make_gate(work[:, FAR : FAR + 512], far_acc[:])
+        product(slice(0, LEAD), work[:, FAR + 224 : FAR + 288], work[:, G0 : G0 + LEAD])
+        make_gate(work[:, FAR : FAR + 256], far_acc[:, 0:256])
+        make_gate(work[:, FAR + 256 : FAR + 512], next_acc[:, 0:256])
         far_acc = psum.tile([P, 512], F32, name="far_acc1", tag="far_bank")
-        multiply(far_acc, 1, second, (0, 1))
+        multiply(far_acc, 1, [slice(640, 768), quarters[3]], (0, 1))
         make_gate(work[:, 256:512], near_acc[2][:, 0:256])
-        product(slice(LEAD, 256), work[:, OLD + LEAD : OLD + 256], work[:, G0 + LEAD : G0 + 256])
+        product(slice(LEAD, 256), work[:, MID + LEAD : MID + 256], work[:, G0 + LEAD : G0 + 256])
         make_gate(work[:, 512:768], near_acc[3][:, 0:256])
+        make_gate(work[:, FAR + 512 : FAR + 640], early_acc[:, 0:128])
         product(slice(256, SHARE), work[:, OLD + 256 : OLD + SHARE], work[:, 0 : SHARE - 256])
         put_scalar(slice(0, 256))
         product(slice(SHARE, S), work[:, OLD + SHARE : OLD + S], work[:, SHARE - 256 : 768])
-        make_gate(work[:, FAR + 512 : FAR + S], far_acc[:])
+        make_gate(work[:, FAR + 640 : FAR + S], far_acc[:, 0:384])
         put_scalar(slice(256, S))
         nc.sync.dma_start(out[0:P, :], near[:])
         fetch_vector(old_far[:], 1, slice(0, S))

@@ -163,7 +163,7 @@ def tile_picked_idxput_gate_p_kernel(tc, x_words, x_scales, mem, w1, offs, slot,
             nc.scalar.activation(near[:].indirect(slot_sb[:, columns(entries)]), new_near[:, entries], ACT.Copy, scale=ones[:])
 
         LEAD = 64
-        SHARE = 320
+        SHARE = 384
         FAR = 768
         OLD = FAR + S - 256
         MID = FAR + 544 - LEAD

from contextlib import ExitStack

import concourse.mybir as mybir

K, T, S, N, U = 1024, 2048, 1024, 256, 2048
FLOPS = 2 * K * S * N

F32 = mybir.dt.float32
BF16 = mybir.dt.bfloat16
I32 = mybir.dt.int32
U32 = mybir.dt.uint32
U16 = mybir.dt.uint16
U8 = mybir.dt.uint8
FP8X4 = mybir.dt.float8_e4m3fn_x4
FP4X4 = mybir.dt.float4_e2m1fn_x4
ACT = mybir.ActivationFunctionType
MULT = mybir.AluOpType.mult
ADD = mybir.AluOpType.add

P = 128
PACK = 4
K_PASS = P * PACK
PASSES = K // K_PASS
QUADRANT = 32
QUADRANTS = P // QUADRANT
SCALE_ROWS = 4
TABLE_START = P - PASSES * QUADRANTS * SCALE_ROWS


def tile_picked_idxput_gate_p_kernel(tc, x_words, x_scales, mem, w1, offs, slot, out):
    nc = tc.nc
    with ExitStack() as ctx:
        keep = ctx.enter_context(tc.tile_pool(name="keep", bufs=1))
        rows_pool = ctx.enter_context(tc.tile_pool(name="rows_pool", bufs=1))
        late_pool = ctx.enter_context(tc.tile_pool(name="late_pool", bufs=1))
        psum = ctx.enter_context(tc.psum_pool(name="psum", bufs=1))

        def columns(entries):
            return slice(entries.start // 16, entries.stop // 16)

        offs_sb = keep.tile([P, S // 16], U16, name="offs_sb")
        slot_sb = keep.tile([P, S // 16], U16, name="slot_sb")
        row_bytes = 4 * U
        scale_table = rows_pool.tile([P, T], U8, name="scale_table", offset=row_bytes - T // 2, align_bytes=256)
        word_table = [
            keep.tile([P, 4 * S], U16, name="word_table0", align_bytes=256),
            keep.tile([P, T], U16, name="word_table1", align_bytes=256),
        ]
        picked_scales = late_pool.tile([P, S], U8, name="picked_scales", offset=0, align_bytes=256)
        x_scale = keep.tile([P, PASSES * S], U8, name="x_scale", align_bytes=256)
        nc.vector.memset(scale_table[0:TABLE_START, :].bitcast(I32), 0)
        nc.vector.memset(x_scale[:].bitcast(I32), 0)
        ones = keep.tile([P, 1], F32, name="ones", align_bytes=64)
        nc.vector.memset(ones[:], 1.0)

        w_raw = [keep.tile([P, PACK, N], F32, name=f"w_raw{z}", tag=f"w_raw{z}", align_bytes=256) for z in range(PASSES)]
        nc.sync.dma_start(scale_table[TABLE_START:P, :].bitcast(I32), x_scales.rearrange("z i c -> i z c").bitcast(I32))
        nc.sync.dma_start(offs_sb[:], offs)
        nc.sync.dma_start(word_table[0][:, 0:T].bitcast(I32), x_words[0].bitcast(I32))
        for z in range(PASSES):
            nc.sync.dma_start(w_raw[z][:], w1[z * K_PASS : (z + 1) * K_PASS, :].rearrange("(p t) n -> p t n", t=PACK))
        nc.sync.dma_start(word_table[1][:].bitcast(I32), x_words[1].bitcast(I32))
        nc.sync.dma_start(slot_sb[:], slot)

        nc.vector.tensor_copy(picked_scales[:], scale_table[:].indirect(offs_sb[:]))
        for q in (0, 2, 1, 3):
            start = TABLE_START + q * SCALE_ROWS * PASSES
            rows = x_scale[q * QUADRANT : q * QUADRANT + SCALE_ROWS, :]
            nc.sync.dma_start(
                rows.rearrange("r (z c) -> r z c", z=PASSES).bitcast(I32),
                picked_scales[start : start + SCALE_ROWS * PASSES, :].bitcast(I32),
            )
        near = rows_pool.tile([P, U], F32, name="near", offset=0, align_bytes=256)
        far = rows_pool.tile([P, U], F32, name="far", offset=row_bytes, align_bytes=256)
        nc.sync.dma_start(near[:], mem[0:P, :])
        nc.sync.dma_start(far[:], mem[P : 2 * P, :])

        words0 = keep.tile([P, S], U16, name="words0", align_bytes=64)
        nc.vector.tensor_copy(words0[:], word_table[0][:].indirect(offs_sb[:]))

        grouped = [keep.tile([P, PASSES, P, PACK], BF16, name=f"grouped{b}", tag=f"grouped{b}", align_bytes=64) for b in range(2)]
        warm = keep.tile([P, 1], F32, name="warm", align_bytes=64)
        nc.vector.memset(warm[:], 0.0)
        warmed = keep.tile([P, 1], F32, name="warmed", align_bytes=64)
        nc.scalar.activation(warmed[:], warm[:], ACT.Sigmoid)

        def cast(b, z):
            nc.scalar.copy(
                grouped[b][:, z].rearrange("p (c i) t -> p c t i", i=4),
                w_raw[z][:, :, b * P : (b + 1) * P].rearrange("p t (c i) -> p c t i", i=4),
            )

        cast(0, 0)
        nc.gpsimd.tensor_scalar(grouped[1][:, 0], w_raw[0][:, :, P:N].rearrange("p t m -> p m t"), 1.0, 0.0, MULT, ADD)
        cast(0, 1)
        cast(1, 1)
        w_codes = [keep.tile([P, PASSES * P], U32, name=f"w_codes{b}", tag=f"w_codes{b}", align_bytes=64) for b in range(2)]
        w_scale = [
            keep.tile([P, PASSES * P], U8, name="w_scale0", align_bytes=64),
            keep.tile([P, PASSES * P], U8, name="w_scale1", align_bytes=64),
        ]

        def quantize(b):
            nc.vector.quantize_mx(w_codes[b][:].bitcast(FP8X4), w_scale[b][:], grouped[b][:].rearrange("p z m t -> p (z m t)"))

        first, second = slice(0, 512), slice(512, S)
        quantize(0)
        quarters = [slice(a, a + 256) for a in range(0, S, 256)]
        words1_first = keep.tile([P, 512], U16, name="words1_first", align_bytes=64)
        for entries in quarters[0:2]:
            nc.vector.tensor_copy(words1_first[:, entries], word_table[1][:].indirect(offs_sb[:, columns(entries)]))
        quantize(1)
        words1_second = late_pool.tile([P, 512], U16, name="words1_second", offset=768, align_bytes=256)
        nc.vector.tensor_copy(words1_second[:], word_table[1][:].indirect(offs_sb[:, columns(second)]))

        def words(z, entries):
            if z == 0:
                return words0[:, entries]
            if entries.start < 512:
                return words1_first[:, entries]
            return words1_second[:, entries.start - 512 : entries.stop - 512]

        def multiply(acc, b, parts, order):
            steps = [(z, part) for z in order for part in parts]
            for i, (z, part) in enumerate(steps):
                w_cols = slice(z * P, (z + 1) * P)
                nc.tensor.matmul_mx(
                    out=acc[:, part.start - parts[0].start : part.stop - parts[0].start],
                    lhsT=w_codes[b][:, w_cols].bitcast(FP8X4),
                    lhsT_scale=w_scale[b][:, w_cols],
                    rhs=words(z, part).bitcast(FP4X4),
                    rhs_scale=x_scale[:, z * S + part.start : z * S + part.stop],
                    start=(i == 0),
                    stop=(i == len(steps) - 1),
                )

        near_acc = [psum.tile([P, 512], F32, name=f"near_acc{i}") for i in range(4)]
        far_acc = psum.tile([P, 512], F32, name="far_acc0", tag="far_bank")
        multiply(near_acc[0], 0, [quarters[0]], (0, 1))
        multiply(near_acc[1], 0, [quarters[1]], (0, 1))
        multiply(far_acc, 1, [quarters[0]], (0, 1))
        next_acc = psum.tile([P, 512], F32, name="next_acc")
        multiply(next_acc, 1, [quarters[1]], (0, 1))
        multiply(near_acc[2], 0, [quarters[2]], (0, 1))
        multiply(near_acc[3], 0, [quarters[3]], (1, 0))
        early_acc = psum.tile([P, 512], F32, name="early_acc")
        multiply(early_acc, 1, [slice(512, 640)], (0, 1))
        window = [near, far]

        def make_gate(gate, acc):
            nc.scalar.activation(gate, acc, ACT.Sigmoid)

        def fetch_scalar(old, b, entries):
            nc.scalar.activation(old, window[b][:].indirect(slot_sb[:, columns(entries)]), ACT.Copy)

        def fetch_vector(old, b, entries):
            nc.vector.tensor_copy(old, window[b][:].indirect(slot_sb[:, columns(entries)]))

        def product(entries, old, gate):
            nc.gpsimd.tensor_tensor(new_near[:, entries], old, gate, MULT)

        def put_scalar(entries):
            nc.scalar.activation(near[:].indirect(slot_sb[:, columns(entries)]), new_near[:, entries], ACT.Copy, scale=ones[:])

        LEAD = 64
        SHARE = 384
        FAR = 768
        OLD = FAR + S - 256
        MID = FAR + 544 - LEAD
        G0 = 512 - LEAD
        work = keep.tile([P, OLD + S], F32, name="work", align_bytes=64)
        new_near = keep.tile([P, S], F32, name="new_near", align_bytes=64)
        old_far = keep.tile([P, S], F32, name="old_far", align_bytes=64)

        make_gate(work[:, G0 : G0 + 256], near_acc[0][:, 0:256])
        make_gate(work[:, 0:256], near_acc[1][:, 0:256])
        fetch_scalar(work[:, FAR + 224 : FAR + 288], 0, slice(0, LEAD))
        fetch_scalar(work[:, MID + LEAD : MID + 256], 0, slice(LEAD, 256))
        fetch_scalar(work[:, OLD + 256 : OLD + SHARE], 0, slice(256, SHARE))
        fetch_vector(work[:, OLD + SHARE : OLD + S], 0, slice(SHARE, S))
        product(slice(0, LEAD), work[:, FAR + 224 : FAR + 288], work[:, G0 : G0 + LEAD])
        make_gate(work[:, FAR : FAR + 256], far_acc[:, 0:256])
        make_gate(work[:, FAR + 256 : FAR + 512], next_acc[:, 0:256])
        far_acc = psum.tile([P, 512], F32, name="far_acc1", tag="far_bank")
        multiply(far_acc, 1, [slice(640, 768), quarters[3]], (0, 1))
        make_gate(work[:, 256:512], near_acc[2][:, 0:256])
        product(slice(LEAD, 256), work[:, MID + LEAD : MID + 256], work[:, G0 + LEAD : G0 + 256])
        make_gate(work[:, 512:768], near_acc[3][:, 0:256])
        make_gate(work[:, FAR + 512 : FAR + 640], early_acc[:, 0:128])
        product(slice(256, SHARE), work[:, OLD + 256 : OLD + SHARE], work[:, 0 : SHARE - 256])
        put_scalar(slice(0, 256))
        product(slice(SHARE, S), work[:, OLD + SHARE : OLD + S], work[:, SHARE - 256 : 768])
        make_gate(work[:, FAR + 640 : FAR + S], far_acc[:, 0:384])
        put_scalar(slice(256, S))
        nc.sync.dma_start(out[0:P, :], near[:])
        fetch_vector(old_far[:], 1, slice(0, S))
        nc.vector.tensor_tensor(far[:].indirect(slot_sb[:]), old_far[:], work[:, FAR : FAR + S], MULT)
        nc.sync.dma_start(out[P : 2 * P, :], far[:])
